import numpy as np
import ml_dtypes


def mxq(x, axis, fmt="e4m3"):
    dtype, down = {"e4m3": (ml_dtypes.float8_e4m3fn, 7), "e5m2": (ml_dtypes.float8_e5m2, 14)}[fmt]
    v = np.moveaxis(np.asarray(x, np.float32).astype(ml_dtypes.bfloat16).astype(np.float64), axis, -1)
    blocks = v.reshape(v.shape[:-1] + (-1, 32))
    amax = np.abs(blocks).max(-1, keepdims=True)
    byte = np.maximum(np.where(amax > 0, np.frexp(amax)[1] - 1 + 127, 0) - down, 1)
    scale = np.exp2(byte - 127.0)
    codes = (blocks / scale).astype(np.float32).astype(dtype).astype(np.float64)
    return np.moveaxis((codes * scale).reshape(v.shape), -1, axis)


WIDE = False


def mx_kscale(k):
    if not WIDE:
        return np.ones(k)
    levels = np.array([10, -10, 5, -5, 0])
    if k % 512:
        return np.exp2(np.random.permutation(np.resize(levels, k // 32))).repeat(32)
    a = np.empty((k // 512, 16))
    for p in range(k // 512):
        a[p, :8] = np.random.permutation(np.resize(levels, 8))
        for g in range(8):
            far = levels[np.abs(levels - a[p, g]) >= 10]
            a[p, g + 8] = far[np.random.randint(len(far))]
    return np.exp2(a.ravel()).repeat(32)


BF16 = ml_dtypes.bfloat16


def bf(x):
    return np.asarray(x, np.float32).astype(BF16)


def f64(x):
    return np.asarray(x).astype(np.float64)


E2M1 = np.array([0.0, 0.5, 1.0, 1.5, 2.0, 3.0, 4.0, 6.0, -0.0, -0.5, -1.0, -1.5, -2.0, -3.0, -4.0, -6.0])


def pack_weight(w, fmt):
    k, n = w.shape
    w = f64(bf(w)).reshape(k // 32, 32, n)
    amax = np.abs(w).max(1)
    if fmt == "e4m3":
        byte = np.frexp(amax)[1] - 1 + 127 - 7
    else:
        mant, ex = np.frexp(amax / 6.0)
        byte = np.where(mant > 0.5, ex, ex - 1) + 127
    byte = np.clip(np.where(amax > 0, byte, 1), 1, 254)
    scaled = (w * np.exp2(127.0 - byte)[:, None, :]).reshape(k, n).astype(np.float32)
    by_word = np.ascontiguousarray(scaled.reshape(k // 512, 128, 4, n).transpose(0, 1, 3, 2))
    if fmt == "e4m3":
        words = by_word.astype(ml_dtypes.float8_e4m3fn).view(np.uint8)
    else:
        c = by_word.astype(ml_dtypes.float4_e2m1fn).view(np.uint8) & 0xF
        words = c[..., 0::2] | (c[..., 1::2] << 4)
    return np.ascontiguousarray(words), np.ascontiguousarray(byte.astype(np.uint8).reshape(k // 512, 16, n))


def unpack_weight(words, scales, fmt):
    g, p, n, _ = words.shape
    if fmt == "e4m3":
        vals = np.ascontiguousarray(words).view(ml_dtypes.float8_e4m3fn).astype(np.float64)
    else:
        nib = np.empty((g, p, n, 4), np.uint8)
        nib[..., 0::2] = words & 0xF
        nib[..., 1::2] = words >> 4
        vals = E2M1[nib]
    vals = vals * np.repeat(np.exp2(scales.astype(np.float64) - 127.0), 8, axis=1)[..., None]
    return vals.transpose(0, 1, 3, 2).reshape(g * 512, n)

E4M3FN = np.array([(-1.0 if i & 128 else 1.0) * ((1.0 + (i & 7) / 8.0) * 2.0 ** (((i >> 3) & 15) - 7) if i & 120 else (i & 7) * 2.0 ** -9) for i in range(256)])


def e4m3fn_bytes(y):
    return np.clip(np.asarray(y, np.float64), -448.0, 448.0).astype(np.float32).astype(ml_dtypes.float8_e4m3fn).view(np.uint8)


def e4m3fn_values(b):
    return E4M3FN[b]


N, DA, C, F, DB, K = 1024, 512, 512, 1024, 128, 4
J = 3 * K * DB


def sigmoid(v):
    return 1.0 / (1.0 + np.exp(-v))


def softmax(v, axis):
    e = np.exp(v - v.max(axis=axis, keepdims=True))
    return e / e.sum(axis=axis, keepdims=True)


def draw0():
    sa, sc = mx_kscale(DA), mx_kscale(C)
    t = mx_kscale(F)
    xa = bf(np.random.standard_normal((N, DA)) * sa)
    xb = bf(np.random.standard_normal((N, DB)))
    c = bf(np.random.standard_normal((N, C)) * sc)
    wa_words, wa_scales = pack_weight(np.random.standard_normal((DA, F)) / np.sqrt(DA) / sa[:, None] * t, "e4m3")
    wc_words, wc_scales = pack_weight(np.random.standard_normal((C, F)) / np.sqrt(C) / sc[:, None] * t, "e4m3")
    b = bf(0.3 * np.random.standard_normal(F) * t)
    wo_words, wo_scales = pack_weight(np.random.standard_normal((F, J)) / np.sqrt(F) / t[:, None], "e4m3")
    return {
        "xa": xa,
        "xb": xb,
        "c": c,
        "wa_words": wa_words,
        "wa_scales": wa_scales,
        "wc_words": wc_words,
        "wc_scales": wc_scales,
        "b": b,
        "wo_words": wo_words,
        "wo_scales": wo_scales,
    }


def conditioner(xa, c, wa_words, wa_scales, wc_words, wc_scales, b, wo_words, wo_scales):
    a = (mxq(f64(xa), 1, "e4m3") @ unpack_weight(wa_words, wa_scales, "e4m3")) + (mxq(f64(c), 1, "e4m3") @ unpack_weight(wc_words, wc_scales, "e4m3")) + f64(b)[None, :]
    h = np.maximum(a, 0.2 * a)
    return mxq(h, 1, "e4m3") @ unpack_weight(wo_words, wo_scales, "e4m3")


def core(xa, xb, c, wa_words, wa_scales, wc_words, wc_scales, b, wo_words, wo_scales):
    n, db = xb.shape
    groups = wo_words.shape[2] // (K * db)
    p = conditioner(xa, c, wa_words, wa_scales, wc_words, wc_scales, b, wo_words, wo_scales)
    p = np.reshape(p, (n, groups, K, db))
    pl = p[:, 0]
    mu = p[:, 1]
    l = p[:, 2]
    pi = softmax(pl, 1)
    z = (f64(xb)[:, None, :] - mu) * np.exp(-np.tanh(l))
    cdf = np.sum(pi * sigmoid(z), axis=1)
    u = 0.01 + 0.98 * cdf
    return np.log(u) - np.log(1.0 - u)


def setup_inputs():
    drawn = draw0()
    full = np.asarray(drawn['xa']).astype(np.float64)
    scale = (np.abs(full).reshape(8, 128, 4, 128).max(axis=(1, 3)) / 448.0).astype(np.float32)
    given = {}
    for key, value in drawn.items():
        if key == 'xa':
            given['xa_bytes'] = e4m3fn_bytes(full / np.repeat(np.repeat(scale.astype(np.float64), 128, axis=0), 128, axis=1))
            given['xa_scale'] = scale
        else:
            given[key] = value
    return given


def reference(xa_bytes, xa_scale, xb, c, wa_words, wa_scales, wc_words, wc_scales, b, wo_words, wo_scales):
    return core(e4m3fn_values(xa_bytes) * np.repeat(np.repeat(xa_scale.astype(np.float64), 128, axis=0), 128, axis=1), xb, c, wa_words, wa_scales, wc_words, wc_scales, b, wo_words, wo_scales)

@@ -1,0 +1,378 @@
+from contextlib import ExitStack
+
+import concourse.mybir as mybir
+from concourse.masks import make_identity
+
+F32 = mybir.dt.float32
+BF16 = mybir.dt.bfloat16
+I32 = mybir.dt.int32
+U8 = mybir.dt.uint8
+FP8 = mybir.dt.float8_e4m3fn
+FP8X4 = mybir.dt.float8_e4m3fn_x4
+ACT = mybir.ActivationFunctionType
+ALU = mybir.AluOpType
+AX = mybir.AxisListType
+
+P = 128
+TOKENS, D_IN, F, DB, K = 1024, 512, 1024, 128, 4
+J = 3 * K * DB
+HALF = 512
+TILES = TOKENS // P
+HALF_TILES = HALF // P
+PASSES2 = F // 512
+
+Z_ON_GPSIMD = ()
+FLOPS = 2 * TOKENS * (2 * D_IN * F + F * J)
+
+
+def tile_conditionalmixturelogisticcdfcouplingmap_d2p_kernel(
+    tc, xa_bytes, xa_scale, xb, c, wa_words, wa_scales, wc_words, wc_scales, b, wo_words, wo_scales, out
+):
+    nc = tc.nc
+    with ExitStack() as ctx:
+        keep = ctx.enter_context(tc.tile_pool(name="keep", bufs=1))
+        work = ctx.enter_context(tc.tile_pool(name="work", bufs=2))
+        psum = ctx.enter_context(tc.psum_pool(name="psum", bufs=1))
+        ctx.enter_context(tc.manual_schedule())
+
+        def bank(dtype=F32, cols=512):
+            w = psum.tile([P, cols], dtype, name="w", tag="w", bufs=6)
+            return w
+
+        xa_u8 = [keep.tile([P, HALF_TILES * D_IN], U8, name="xa_u8_" + str(h), align_bytes=64) for h in range(2)]
+        c_sb = [keep.tile([P, HALF_TILES * D_IN], BF16, name="c_sb_" + str(h), align_bytes=64) for h in range(2)]
+        xa_bf = [keep.tile([P, HALF_TILES * D_IN], BF16, name="xa_bf_" + str(h), align_bytes=64) for h in range(2)]
+        xb_sb = keep.tile([P, TILES, DB], BF16, name="xb_sb", align_bytes=64)
+        xb_t = keep.tile([P, TOKENS], BF16, name="xb_t", align_bytes=64)
+        w_raw = [keep.tile([P, F], I32, name="w_raw_" + str(o), align_bytes=64) for o in range(2)]
+        w_codes = [keep.tile([P, F], I32, name="w_codes_" + str(o), align_bytes=64) for o in range(2)]
+        w_sc_raw = keep.tile([P, F], U8, name="w_sc_raw", align_bytes=64)
+        w_sc = keep.tile([P, F], U8, name="w_sc", align_bytes=64)
+        wo_codes = [keep.tile([P, J], I32, name="wo_codes_" + str(g), align_bytes=64) for g in range(2)]
+        wo_sc = keep.tile([P, J], U8, name="wo_sc", align_bytes=64)
+        x_codes = [[keep.tile([P, HALF], I32, name="x_codes_" + str(o) + str(h), align_bytes=64) for h in range(2)] for o in range(2)]
+        x_sc = [[keep.tile([P, HALF], U8, name="x_sc_" + str(o) + str(h), align_bytes=64) for h in range(2)] for o in range(2)]
+        h_codes = [[keep.tile([P, HALF], I32, name="h_codes_" + str(g) + str(h), align_bytes=64) for h in range(2)] for g in range(2)]
+        h_sc = [[keep.tile([P, HALF], U8, name="h_sc_" + str(g) + str(h), align_bytes=64) for h in range(2)] for g in range(2)]
+        sc_all = keep.tile([P, 32], F32, name="sc_all")
+        sc_col = keep.tile([P, TILES], F32, name="sc_col")
+        bias_bf = keep.tile([P, PASSES2, 4], BF16, name="bias_bf")
+        bias = keep.tile([P, PASSES2 * 4], F32, name="bias")
+        ident = keep.tile([P, P], F32, name="ident")
+        ident_bf = keep.tile([P, P], BF16, name="ident_bf")
+        ab = keep.tile([P, 2, TOKENS], F32, name="ab")
+        ln_ab = keep.tile([P, 2, TOKENS], F32, name="ln_ab")
+        out_sb = keep.tile([P, TOKENS], F32, name="out_sb")
+        warm = keep.tile([P, 1], F32, name="warm")
+
+        nc.vector.memset(warm[:], 0.0)
+        nc.scalar.activation(out=warm[:], in_=warm[:], func=ACT.Exp)
+        nc.vector.memset(w_sc_raw[:].bitcast(I32), 0)
+        make_identity(nc, ident[:])
+        nc.vector.memset(wo_sc[:].bitcast(I32), 0)
+        nc.vector.tensor_copy(out=ident_bf[:], in_=ident[:])
+
+        xa_rows = xa_bytes.rearrange("(j p) k -> p j k", p=P)
+        c_rows = c.rearrange("(j p) k -> p j k", p=P)
+
+        def load_x(h):
+            tiles = slice(h * HALF_TILES, (h + 1) * HALF_TILES)
+            nc.sync.dma_start(out=xa_u8[h][:].rearrange("p (j k) -> p j k", k=D_IN), in_=xa_rows[:, tiles, :])
+            nc.sync.dma_start(out=c_sb[h][:].rearrange("p (j k) -> p j k", k=D_IN), in_=c_rows[:, tiles, :])
+
+        nc.scalar.dma_start(out=sc_all[:], in_=xa_scale.rearrange("i j -> (i j)").partition_broadcast(P))
+        nc.scalar.dma_start(out=bias_bf[:], in_=b.rearrange("(g p t) -> p g t", p=P, t=4))
+        for q in range(4):
+            nc.scalar.dma_start(
+                out=w_sc_raw[32 * q : 32 * q + 4, :].bitcast(I32), in_=wa_scales[0, 4 * q : 4 * q + 4, :].bitcast(I32)
+            )
+        load_x(0)
+        for o, words in enumerate((wa_words, wc_words)):
+            nc.sync.dma_start(out=w_raw[o][:], in_=words[0].rearrange("p n t -> p (n t)").bitcast(I32))
+        load_x(1)
+        nc.sync.dma_start(out=xb_sb[:], in_=xb.rearrange("(j p) d -> p j d", p=P))
+        for g in range(PASSES2):
+            nc.sync.dma_start(out=wo_codes[g][:], in_=wo_words[g].rearrange("p n t -> p (n t)").bitcast(I32))
+        for q in range(4):
+            nc.gpsimd.dma_start(
+                out=w_sc_raw[32 * q + 4 : 32 * q + 8, :].bitcast(I32), in_=wc_scales[0, 4 * q : 4 * q + 4, :].bitcast(I32)
+            )
+        for g in range(PASSES2):
+            for q in range(4):
+                nc.gpsimd.dma_start(
+                    out=wo_sc[32 * q + 4 * g : 32 * q + 4 * g + 4, :].bitcast(I32),
+                    in_=wo_scales[g, 4 * q : 4 * q + 4, :].bitcast(I32),
+                )
+        for q in range(4):
+            nc.vector.tensor_copy(out=sc_col[32 * q : 32 * q + 32, :], in_=sc_all[32 * q : 32 * q + 32, q::4])
+        nc.vector.tensor_copy(out=bias[:], in_=bias_bf[:].rearrange("p g t -> p (g t)"))
+
+        def cast_xa(h, eng, t0, t1):
+            cols = slice(t0 * D_IN, t1 * D_IN)
+            src = xa_u8[h][:, cols].bitcast(FP8)
+            if eng == "v":
+                nc.vector.tensor_copy(out=xa_bf[h][:, cols], in_=src)
+            else:
+                nc.scalar.copy(out=xa_bf[h][:, cols], in_=src)
+
+        def turn(src, pair):
+            w = bank()
+            words = src[:].bitcast(F32)
+            for jj in range(2):
+                for u in range(2):
+                    base = (2 * pair + jj) * (D_IN // 2)
+                    nc.tensor.transpose(
+                        w[:, (2 * jj + u) * P : (2 * jj + u + 1) * P], words[:, base + u : base + D_IN // 2 : 2], ident[:]
+                    )
+            return w
+
+        x_in = {}
+
+        def new_in(name):
+            x_in[name] = work.tile([P, 4 * HALF], BF16, name="grouped", tag="grouped", bufs=4, align_bytes=64)
+            return x_in[name]
+
+        def empty_xa(h, pair, w):
+            for jj in range(2):
+                j = 2 * pair + jj
+                src = w[:, 2 * jj * P : (2 * jj + 2) * P].bitcast(BF16).rearrange("p (u n e) -> p n u e", u=2, e=2)
+                dst = x_in["xa", h][:, j * D_IN : (j + 1) * D_IN].rearrange("p (n u e) -> p n u e", u=2, e=2)
+                jt = h * HALF_TILES + j
+                nc.vector.tensor_scalar(out=dst, in0=src, scalar1=sc_col[:, jt : jt + 1], scalar2=None, op0=ALU.mult)
+
+        def empty_c(h, pair, w):
+            dst = x_in["c", h][:, 2 * pair * D_IN : (2 * pair + 2) * D_IN].bitcast(F32)
+            nc.scalar.copy(
+                out=dst.rearrange("p (j n u) -> p j n u", j=2, u=2), in_=w[:].rearrange("p (j u n) -> p j n u", j=2, u=2)
+            )
+
+        def quantize(src, codes, scales):
+            nc.vector.quantize_mx(out=codes[:].bitcast(FP8X4), scales=scales[:], in_=src[:])
+
+        def permute(o, g):
+            cols = slice(512 * g, 512 * g + 512)
+            nc.vector.tensor_copy(
+                out=w_codes[o][:, cols].rearrange("p (t m) -> p t m", t=4), in_=w_raw[o][:, cols].rearrange("p (m t) -> p t m", t=4)
+            )
+
+        def permute_scales(g):
+            cols = slice(512 * g, 512 * g + 512)
+            nc.vector.tensor_copy(
+                out=w_sc[:, cols].rearrange("p (t m) -> p t m", t=4), in_=w_sc_raw[:, cols].rearrange("p (m t) -> p t m", t=4)
+            )
+
+        y_of = {}
+
+        def stage1(h, g):
+            y = work.tile([P, 4, HALF], F32, name="y", tag="y", bufs=2)
+            y_of[h, g] = y
+            for t in range(4):
+                w = bank()
+                cols = slice((4 * g + t) * P, (4 * g + t + 1) * P)
+                for o in range(2):
+                    nc.tensor.matmul_mx(
+                        out=w[:],
+                        lhsT=w_codes[o][:, cols].bitcast(FP8X4),
+                        lhsT_scale=w_sc[4 * o : P, cols],
+                        rhs=x_codes[o][h][:].bitcast(FP8X4),
+                        rhs_scale=x_sc[o][h][:],
+                        start=(o == 0),
+                        stop=(o == 1),
+                    )
+                nc.scalar.activation(out=y[:, t, :], in_=w[:], func=ACT.Identity, bias=bias[:, 4 * g + t : 4 * g + t + 1])
+
+        def leaky(h, g):
+            y = y_of.pop((h, g))
+            grouped = new_in(("h", g, h))
+            yv = y[:].rearrange("p t n -> p n t")
+            nc.vector.scalar_tensor_tensor(
+                out=grouped[:].rearrange("p (n t) -> p n t", t=4), in0=yv, scalar=0.2, in1=yv, op0=ALU.mult, op1=ALU.max
+            )
+
+        def quantize_h(h, g):
+            quantize(x_in.pop(("h", g, h)), h_codes[g][h], h_sc[g][h])
+
+        st = {}
+
+        def stage2(j):
+            h, jj = divmod(j, HALF_TILES)
+            toks = slice(jj * P, (jj + 1) * P)
+            for name, grp in (("l", 2), ("mu", 1), ("pl", 0)):
+                w = bank()
+                st[name, j] = w
+                for k in range(K):
+                    cols = slice(grp * 512 + k * P, grp * 512 + (k + 1) * P)
+                    for g in range(PASSES2):
+                        nc.tensor.matmul_mx(
+                            out=w[:, k * P : (k + 1) * P],
+                            lhsT=wo_codes[g][:, cols].bitcast(FP8X4),
+                            lhsT_scale=wo_sc[4 * g : P, cols],
+                            rhs=h_codes[g][h][:, toks].bitcast(FP8X4),
+                            rhs_scale=h_sc[g][h][:, toks],
+                            start=(g == 0),
+                            stop=(g == PASSES2 - 1),
+                        )
+
+        def sb(name, j, bufs=3):
+            t = work.tile([P, K * DB], F32, name=name, tag=name, bufs=bufs)
+            st[name, j] = t
+            return t
+
+        def a_tanh(j):
+            nc.scalar.activation(out=sb("t", j)[:], in_=st.pop(("l", j))[:], func=ACT.Tanh)
+
+        def a_exp(j):
+            nc.scalar.activation(out=sb("s", j)[:], in_=st.pop(("t", j))[:], func=ACT.Exp, scale=-1.0)
+
+        def v_diff(j):
+            x3 = xb_t[:, j * P : (j + 1) * P].unsqueeze(1).to_broadcast([P, K, P])
+            nc.vector.tensor_tensor(
+                out=sb("d", j)[:].rearrange("p (k n) -> p k n", k=K),
+                in0=st.pop(("mu", j))[:].rearrange("p (k n) -> p k n", k=K),
+                in1=x3,
+                op=ALU.subtract,
+            )
+
+        def v_max(j):
+            m = work.tile([P, P], F32, name="m", tag="m", bufs=2)
+            st["m", j] = m
+            nc.vector.tensor_reduce(out=m[:], in_=st["pl", j][:].rearrange("p (k n) -> p n k", k=K), axis=AX.X, op=ALU.max)
+
+        def v_sub(j):
+            m3 = st.pop(("m", j))[:].unsqueeze(1).to_broadcast([P, K, P])
+            nc.vector.tensor_tensor(
+                out=sb("q", j)[:].rearrange("p (k n) -> p k n", k=K),
+                in0=st.pop(("pl", j))[:].rearrange("p (k n) -> p k n", k=K),
+                in1=m3,
+                op=ALU.subtract,
+            )
+
+        def v_z(j, eng):
+            eng.tensor_tensor(out=sb("z", j)[:], in0=st.pop(("d", j))[:], in1=st.pop(("s", j))[:], op=ALU.mult)
+
+        def a_e(j):
+            nc.scalar.activation(out=sb("e", j)[:], in_=st.pop(("q", j))[:], func=ACT.Exp)
+
+        def a_T(j):
+            nc.scalar.activation(out=sb("T", j)[:], in_=st.pop(("z", j))[:], func=ACT.Tanh, scale=-0.5)
+
+        def v_eT(j, eng):
+            eng.tensor_tensor(out=sb("v", j)[:], in0=st["e", j][:], in1=st.pop(("T", j))[:], op=ALU.mult)
+
+        def sums(j):
+            if j % 2 == 0:
+                st["ev", j // 2] = psum.tile([P, 2, 2, P], F32, name="ev", tag="ev", bufs=2)
+            ev = st["ev", j // 2]
+            for i, name in enumerate(("e", "v")):
+                src = st.pop((name, j))
+                for k in range(K):
+                    nc.tensor.matmul(
+                        ev[:, j % 2, i, :],
+                        lhsT=src[:, k * P : (k + 1) * P],
+                        rhs=ident[:],
+                        is_transpose=True,
+                        start=(k == 0),
+                        stop=(k == K - 1),
+                    )
+
+        def finish_pair(pr):
+            ev = st.pop(("ev", pr))
+            es = work.tile([P, 2, P], F32, name="es", tag="es", bufs=2)
+            cols = slice(2 * pr * P, (2 * pr + 2) * P)
+            if pr < 2:
+                nc.scalar.activation(out=es[:], in_=ev[:, :, 0, :], func=ACT.Copy, scale=1.0 / 0.98)
+            else:
+                nc.vector.tensor_scalar(out=es[:], in0=ev[:, :, 0, :], scalar1=1.0 / 0.98, scalar2=None, op0=ALU.mult)
+            a = ab[:, 0, cols].rearrange("p (j d) -> p j d", j=2)
+            bb = ab[:, 1, cols].rearrange("p (j d) -> p j d", j=2)
+            nc.vector.tensor_tensor(out=a, in0=ev[:, :, 1, :], in1=es[:], op=ALU.add)
+            nc.vector.tensor_tensor(out=bb, in0=es[:], in1=ev[:, :, 1, :], op=ALU.subtract)
+
+        out_rows = out.rearrange("(j p) d -> p j d", p=P)
+
+        def logs(p0, p1):
+            cols = slice(2 * p0 * P, 2 * p1 * P)
+            nc.scalar.activation(out=ln_ab[:, :, cols], in_=ab[:, :, cols], func=ACT.Ln)
+
+        def write_out(p0, p1):
+            cols = slice(2 * p0 * P, 2 * p1 * P)
+            nc.vector.tensor_tensor(out=out_sb[:, cols], in0=ln_ab[:, 0, cols], in1=ln_ab[:, 1, cols], op=ALU.subtract)
+            nc.sync.dma_start(
+                out=out_rows[:, 2 * p0 : 2 * p1, :], in_=out_sb[:, cols].rearrange("p (j d) -> p j d", d=DB)
+            )
+
+        def prep_xa(h):
+            new_in(("xa", h))
+            cast_xa(h, "v", 0, 2 + 2 * h)
+            if h == 0:
+                cast_xa(h, "s", 2, 4)
+            for pair in range(2):
+                empty_xa(h, pair, turn(xa_bf[h], pair))
+            quantize(x_in.pop(("xa", h)), x_codes[0][h], x_sc[0][h])
+
+        def prep_c(h):
+            new_in(("c", h))
+            for pair in range(2):
+                empty_c(h, pair, turn(c_sb[h], pair))
+
+        def quant_c(h):
+            quantize(x_in.pop(("c", h)), x_codes[1][h], x_sc[1][h])
+
+        prep_xa(0)
+        permute(0, 0)
+        prep_c(0)
+        permute_scales(0)
+        permute(1, 0)
+        quant_c(0)
+        permute(0, 1)
+        permute(1, 1)
+        permute_scales(1)
+        stage1(0, 0)
+        prep_xa(1)
+        leaky(0, 0)
+        prep_c(1)
+        quantize_h(0, 0)
+        quant_c(1)
+        stage1(0, 1)
+        leaky(0, 1)
+        wx = bank(BF16, 1024)
+        for j in range(TILES):
+            nc.tensor.transpose(wx[:, j * P : (j + 1) * P], xb_sb[:, j, :], ident_bf[:])
+        nc.scalar.copy(out=xb_t[:], in_=wx[:])
+        quantize_h(0, 1)
+        stage1(1, 0)
+        leaky(1, 0)
+        stage1(1, 1)
+        quantize_h(1, 0)
+        stage2(0)
+        leaky(1, 1)
+        stage2(1)
+        quantize_h(1, 1)
+        for i in range(TILES + 2):
+            if 1 <= i < TILES - 1:
+                stage2(i + 1)
+            if i < TILES:
+                v_diff(i)
+                a_tanh(i)
+                v_max(i)
+                a_exp(i)
+                v_sub(i)
+                v_z(i, nc.gpsimd if i in Z_ON_GPSIMD else nc.vector)
+            if 1 <= i <= TILES:
+                a_e(i - 1)
+                a_T(i - 1)
+                if i == TILES:
+                    finish_pair(2)
+                v_eT(i - 1, nc.vector if i == TILES else nc.gpsimd)
+            if 2 <= i <= TILES + 1:
+                sums(i - 2)
+            if i >= 4 and i % 2 == 0 and i < TILES:
+                finish_pair((i - 4) // 2)
+            if i == TILES:
+                nc.scalar.activation(out=warm[:], in_=warm[:], func=ACT.Ln)
+                logs(0, 3)
+            if i == TILES + 1:
+                finish_pair(3)
+                logs(3, 4)
+                write_out(0, 3)
+        write_out(3, 4)

@@ -65,44 +65,50 @@ def tile_conditionalmixturelogisticcdfcouplingmap_d2p_kernel(
         out_sb = keep.tile([P, TOKENS], F32, name="out_sb")
         warm = keep.tile([P, 1], F32, name="warm")
 
-        nc.vector.memset(warm[:], 0.0)
-        nc.scalar.activation(out=warm[:], in_=warm[:], func=ACT.Exp)
-        nc.vector.memset(w_sc_raw[:].bitcast(I32), 0)
-        make_identity(nc, ident[:])
-        nc.vector.memset(wo_sc[:].bitcast(I32), 0)
-        nc.vector.tensor_copy(out=ident_bf[:], in_=ident[:])
-
         xa_rows = xa_bytes.rearrange("(j p) k -> p j k", p=P)
         c_rows = c.rearrange("(j p) k -> p j k", p=P)
 
-        def load_x(h):
+        def load_xa(h):
             tiles = slice(h * HALF_TILES, (h + 1) * HALF_TILES)
             nc.sync.dma_start(out=xa_u8[h][:].rearrange("p (j k) -> p j k", k=D_IN), in_=xa_rows[:, tiles, :])
+
+        def load_c(h):
+            tiles = slice(h * HALF_TILES, (h + 1) * HALF_TILES)
             nc.sync.dma_start(out=c_sb[h][:].rearrange("p (j k) -> p j k", k=D_IN), in_=c_rows[:, tiles, :])
 
+        def load_words(tile, words):
+            nc.sync.dma_start(out=tile[:], in_=words.rearrange("p n t -> p (n t)").bitcast(I32))
+
+        def load_scales(queue, tile, scales, first, q):
+            rows = slice(32 * q + first, 32 * q + first + 4)
+            queue.dma_start(out=tile[rows, :].bitcast(I32), in_=scales[4 * q : 4 * q + 4, :].bitcast(I32))
+
+        nc.vector.memset(w_sc_raw[:].bitcast(I32), 0)
+        nc.vector.memset(wo_sc[:].bitcast(I32), 0)
+        nc.vector.memset(warm[:], 1.0)
+        make_identity(nc, ident[:])
+        load_xa(0)
+        load_c(0)
+        load_words(w_raw[0], wa_words[0])
+        load_words(w_raw[1], wc_words[0])
         nc.scalar.dma_start(out=sc_all[:], in_=xa_scale.rearrange("i j -> (i j)").partition_broadcast(P))
         nc.scalar.dma_start(out=bias_bf[:], in_=b.rearrange("(g p t) -> p g t", p=P, t=4))
+        load_scales(nc.scalar, w_sc_raw, wa_scales[0], 0, 0)
+        load_scales(nc.scalar, w_sc_raw, wa_scales[0], 0, 1)
+        nc.scalar.activation(out=warm[:], in_=warm[:], func=ACT.Exp)
+        load_scales(nc.sync, w_sc_raw, wa_scales[0], 0, 2)
+        load_scales(nc.sync, w_sc_raw, wa_scales[0], 0, 3)
         for q in range(4):
-            nc.scalar.dma_start(
-                out=w_sc_raw[32 * q : 32 * q + 4, :].bitcast(I32), in_=wa_scales[0, 4 * q : 4 * q + 4, :].bitcast(I32)
-            )
-        load_x(0)
-        for o, words in enumerate((wa_words, wc_words)):
-            nc.sync.dma_start(out=w_raw[o][:], in_=words[0].rearrange("p n t -> p (n t)").bitcast(I32))
-        load_x(1)
+            load_scales(nc.gpsimd, w_sc_raw, wc_scales[0], 4, q)
+        load_xa(1)
+        load_c(1)
         nc.sync.dma_start(out=xb_sb[:], in_=xb.rearrange("(j p) d -> p j d", p=P))
         for g in range(PASSES2):
-            nc.sync.dma_start(out=wo_codes[g][:], in_=wo_words[g].rearrange("p n t -> p (n t)").bitcast(I32))
-        for q in range(4):
-            nc.gpsimd.dma_start(
-                out=w_sc_raw[32 * q + 4 : 32 * q + 8, :].bitcast(I32), in_=wc_scales[0, 4 * q : 4 * q + 4, :].bitcast(I32)
-            )
+            load_words(wo_codes[g], wo_words[g])
         for g in range(PASSES2):
             for q in range(4):
-                nc.gpsimd.dma_start(
-                    out=wo_sc[32 * q + 4 * g : 32 * q + 4 * g + 4, :].bitcast(I32),
-                    in_=wo_scales[g, 4 * q : 4 * q + 4, :].bitcast(I32),
-                )
+                load_scales(nc.gpsimd, wo_sc, wo_scales[g], 4 * g, q)
+        nc.vector.tensor_copy(out=ident_bf[:], in_=ident[:])
         for q in range(4):
             nc.vector.tensor_copy(out=sc_col[32 * q : 32 * q + 32, :], in_=sc_all[32 * q : 32 * q + 32, q::4])
         nc.vector.tensor_copy(out=bias[:], in_=bias_bf[:].rearrange("p g t -> p (g t)"))
@@ -132,13 +138,16 @@ def tile_conditionalmixturelogisticcdfcouplingmap_d2p_kernel(
             x_in[name] = work.tile([P, 4 * HALF], BF16, name="grouped", tag="grouped", bufs=4, align_bytes=64)
             return x_in[name]
 
-        def empty_xa(h, pair, w):
+        def empty_xa(h, pair, w, on_scalar):
             for jj in range(2):
                 j = 2 * pair + jj
                 src = w[:, 2 * jj * P : (2 * jj + 2) * P].bitcast(BF16).rearrange("p (u n e) -> p n u e", u=2, e=2)
                 dst = x_in["xa", h][:, j * D_IN : (j + 1) * D_IN].rearrange("p (n u e) -> p n u e", u=2, e=2)
                 jt = h * HALF_TILES + j
-                nc.vector.tensor_scalar(out=dst, in0=src, scalar1=sc_col[:, jt : jt + 1], scalar2=None, op0=ALU.mult)
+                if on_scalar:
+                    nc.scalar.activation(out=dst, in_=src, func=ACT.Copy, scale=sc_col[:, jt : jt + 1])
+                else:
+                    nc.vector.tensor_scalar(out=dst, in0=src, scalar1=sc_col[:, jt : jt + 1], scalar2=None, op0=ALU.mult)
 
         def empty_c(h, pair, w):
             dst = x_in["c", h][:, 2 * pair * D_IN : (2 * pair + 2) * D_IN].bitcast(F32)
@@ -213,7 +222,7 @@ def tile_conditionalmixturelogisticcdfcouplingmap_d2p_kernel(
                             stop=(g == PASSES2 - 1),
                         )
 
-        def sb(name, j, bufs=3):
+        def sb(name, j, bufs=4):
             t = work.tile([P, K * DB], F32, name=name, tag=name, bufs=bufs)
             st[name, j] = t
             return t
@@ -248,7 +257,7 @@ def tile_conditionalmixturelogisticcdfcouplingmap_d2p_kernel(
             )
 
         def v_z(j, eng):
-            eng.tensor_tensor(out=sb("z", j)[:], in0=st.pop(("d", j))[:], in1=st.pop(("s", j))[:], op=ALU.mult)
+            eng.tensor_tensor(out=sb("z", j)[:], in0=st["d", j][:], in1=st.pop(("s", j))[:], op=ALU.mult)
 
         def a_e(j):
             nc.scalar.activation(out=sb("e", j)[:], in_=st.pop(("q", j))[:], func=ACT.Exp)
@@ -256,8 +265,9 @@ def tile_conditionalmixturelogisticcdfcouplingmap_d2p_kernel(
         def a_T(j):
             nc.scalar.activation(out=sb("T", j)[:], in_=st.pop(("z", j))[:], func=ACT.Tanh, scale=-0.5)
 
-        def v_eT(j, eng):
-            eng.tensor_tensor(out=sb("v", j)[:], in0=st["e", j][:], in1=st.pop(("T", j))[:], op=ALU.mult)
+        def v_eT(j, eng, into):
+            st["v", j] = st.pop(("d", into))
+            eng.tensor_tensor(out=st["v", j][:], in0=st["e", j][:], in1=st.pop(("T", j))[:], op=ALU.mult)
 
         def sums(j):
             if j % 2 == 0:
@@ -303,11 +313,10 @@ def tile_conditionalmixturelogisticcdfcouplingmap_d2p_kernel(
 
         def prep_xa(h):
             new_in(("xa", h))
-            cast_xa(h, "v", 0, 2 + 2 * h)
-            if h == 0:
-                cast_xa(h, "s", 2, 4)
             for pair in range(2):
-                empty_xa(h, pair, turn(xa_bf[h], pair))
+                empty_xa(h, pair, turn(xa_bf[h], pair), pair == 1)
+
+        def quant_xa(h):
             quantize(x_in.pop(("xa", h)), x_codes[0][h], x_sc[0][h])
 
         def prep_c(h):
@@ -318,9 +327,12 @@ def tile_conditionalmixturelogisticcdfcouplingmap_d2p_kernel(
         def quant_c(h):
             quantize(x_in.pop(("c", h)), x_codes[1][h], x_sc[1][h])
 
+        cast_xa(0, "v", 0, 2)
+        cast_xa(0, "s", 2, 4)
         prep_xa(0)
-        permute(0, 0)
         prep_c(0)
+        permute(0, 0)
+        quant_xa(0)
         permute_scales(0)
         permute(1, 0)
         quant_c(0)
@@ -328,12 +340,15 @@ def tile_conditionalmixturelogisticcdfcouplingmap_d2p_kernel(
         permute(1, 1)
         permute_scales(1)
         stage1(0, 0)
-        prep_xa(1)
-        leaky(0, 0)
-        prep_c(1)
-        quantize_h(0, 0)
-        quant_c(1)
+        cast_xa(1, "v", 0, 2)
+        cast_xa(1, "s", 2, 4)
         stage1(0, 1)
+        leaky(0, 0)
+        prep_xa(1)
+        quantize_h(0, 0)
+        prep_c(1)
+        quant_xa(1)
+        quant_c(1)
         leaky(0, 1)
         wx = bank(BF16, 1024)
         for j in range(TILES):
@@ -343,36 +358,46 @@ def tile_conditionalmixturelogisticcdfcouplingmap_d2p_kernel(
         stage1(1, 0)
         leaky(1, 0)
         stage1(1, 1)
-        quantize_h(1, 0)
         stage2(0)
+        a_tanh(0)
+        a_exp(0)
+        v_max(0)
+        quantize_h(1, 0)
         leaky(1, 1)
-        stage2(1)
+        v_diff(0)
+        v_sub(0)
         quantize_h(1, 1)
-        for i in range(TILES + 2):
-            if 1 <= i < TILES - 1:
+        v_z(0, nc.vector)
+        stage2(1)
+        a_tanh(1)
+        a_exp(1)
+        for i in range(1, TILES):
+            if i + 1 < TILES:
                 stage2(i + 1)
-            if i < TILES:
-                v_diff(i)
-                a_tanh(i)
-                v_max(i)
-                a_exp(i)
-                v_sub(i)
-                v_z(i, nc.gpsimd if i in Z_ON_GPSIMD else nc.vector)
-            if 1 <= i <= TILES:
-                a_e(i - 1)
-                a_T(i - 1)
-                if i == TILES:
-                    finish_pair(2)
-                v_eT(i - 1, nc.vector if i == TILES else nc.gpsimd)
-            if 2 <= i <= TILES + 1:
+            v_max(i)
+            v_diff(i)
+            a_e(i - 1)
+            v_sub(i)
+            a_T(i - 1)
+            v_z(i, nc.vector)
+            if i + 1 < TILES:
+                a_tanh(i + 1)
+                a_exp(i + 1)
+            v_eT(i - 1, nc.gpsimd if i < TILES - 1 else nc.vector, i)
+            if i >= 3 and i % 2 == 1:
+                sums(i - 3)
                 sums(i - 2)
-            if i >= 4 and i % 2 == 0 and i < TILES:
+            if i >= 4 and i % 2 == 0:
                 finish_pair((i - 4) // 2)
-            if i == TILES:
-                nc.scalar.activation(out=warm[:], in_=warm[:], func=ACT.Ln)
-                logs(0, 3)
-            if i == TILES + 1:
-                finish_pair(3)
-                logs(3, 4)
-                write_out(0, 3)
+        a_e(TILES - 1)
+        a_T(TILES - 1)
+        nc.scalar.activation(out=warm[:], in_=warm[:], func=ACT.Ln)
+        sums(TILES - 2)
+        finish_pair(2)
+        v_eT(TILES - 1, nc.vector, 0)
+        sums(TILES - 1)
+        logs(0, 3)
+        finish_pair(3)
+        logs(3, 4)
+        write_out(0, 3)
         write_out(3, 4)

@@ -21,7 +21,9 @@ TILES = TOKENS // P
 HALF_TILES = HALF // P
 PASSES2 = F // 512
 
-Z_ON_GPSIMD = ()
+Z_ON_GPSIMD = (2, 3)
+V_ON_GPSIMD = (0, 1)
+C_ON_VECTOR = ((0, 0),)
 FLOPS = 2 * TOKENS * (2 * D_IN * F + F * J)
 
 
@@ -87,19 +89,18 @@ def tile_conditionalmixturelogisticcdfcouplingmap_d2p_kernel(
         nc.vector.memset(wo_sc[:].bitcast(I32), 0)
         nc.vector.memset(warm[:], 1.0)
         make_identity(nc, ident[:])
+        nc.scalar.dma_start(out=sc_all[:], in_=xa_scale.rearrange("i j -> (i j)").partition_broadcast(P))
+        nc.scalar.dma_start(out=bias_bf[:], in_=b.rearrange("(g p t) -> p g t", p=P, t=4))
+        for q in range(3):
+            load_scales(nc.scalar, w_sc_raw, wa_scales[0], 0, q)
         load_xa(0)
         load_c(0)
         load_words(w_raw[0], wa_words[0])
-        load_words(w_raw[1], wc_words[0])
-        nc.scalar.dma_start(out=sc_all[:], in_=xa_scale.rearrange("i j -> (i j)").partition_broadcast(P))
-        nc.scalar.dma_start(out=bias_bf[:], in_=b.rearrange("(g p t) -> p g t", p=P, t=4))
-        load_scales(nc.scalar, w_sc_raw, wa_scales[0], 0, 0)
-        load_scales(nc.scalar, w_sc_raw, wa_scales[0], 0, 1)
         nc.scalar.activation(out=warm[:], in_=warm[:], func=ACT.Exp)
-        load_scales(nc.sync, w_sc_raw, wa_scales[0], 0, 2)
         load_scales(nc.sync, w_sc_raw, wa_scales[0], 0, 3)
         for q in range(4):
-            load_scales(nc.gpsimd, w_sc_raw, wc_scales[0], 4, q)
+            load_scales(nc.sync, w_sc_raw, wc_scales[0], 4, q)
+        load_words(w_raw[1], wc_words[0])
         load_xa(1)
         load_c(1)
         nc.sync.dma_start(out=xb_sb[:], in_=xb.rearrange("(j p) d -> p j d", p=P))
@@ -107,7 +108,7 @@ def tile_conditionalmixturelogisticcdfcouplingmap_d2p_kernel(
             load_words(wo_codes[g], wo_words[g])
         for g in range(PASSES2):
             for q in range(4):
-                load_scales(nc.gpsimd, wo_sc, wo_scales[g], 4 * g, q)
+                load_scales(nc.sync, wo_sc, wo_scales[g], 4 * g, q)
         nc.vector.tensor_copy(out=ident_bf[:], in_=ident[:])
         for q in range(4):
             nc.vector.tensor_copy(out=sc_col[32 * q : 32 * q + 32, :], in_=sc_all[32 * q : 32 * q + 32, q::4])
@@ -151,9 +152,12 @@ def tile_conditionalmixturelogisticcdfcouplingmap_d2p_kernel(
 
         def empty_c(h, pair, w):
             dst = x_in["c", h][:, 2 * pair * D_IN : (2 * pair + 2) * D_IN].bitcast(F32)
-            nc.scalar.copy(
-                out=dst.rearrange("p (j n u) -> p j n u", j=2, u=2), in_=w[:].rearrange("p (j u n) -> p j n u", j=2, u=2)
-            )
+            dst = dst.rearrange("p (j n u) -> p j n u", j=2, u=2)
+            src = w[:].rearrange("p (j u n) -> p j n u", j=2, u=2)
+            if (h, pair) in C_ON_VECTOR:
+                nc.vector.tensor_copy(out=dst, in_=src)
+            else:
+                nc.scalar.copy(out=dst, in_=src)
 
         def quantize(src, codes, scales):
             nc.vector.quantize_mx(out=codes[:].bitcast(FP8X4), scales=scales[:], in_=src[:])
@@ -172,23 +176,35 @@ def tile_conditionalmixturelogisticcdfcouplingmap_d2p_kernel(
 
         y_of = {}
 
-        def stage1(h, g):
-            y = work.tile([P, 4, HALF], F32, name="y", tag="y", bufs=2)
-            y_of[h, g] = y
-            for t in range(4):
-                w = bank()
-                cols = slice((4 * g + t) * P, (4 * g + t + 1) * P)
-                for o in range(2):
-                    nc.tensor.matmul_mx(
-                        out=w[:],
-                        lhsT=w_codes[o][:, cols].bitcast(FP8X4),
-                        lhsT_scale=w_sc[4 * o : P, cols],
-                        rhs=x_codes[o][h][:].bitcast(FP8X4),
-                        rhs_scale=x_sc[o][h][:],
-                        start=(o == 0),
-                        stop=(o == 1),
-                    )
-                nc.scalar.activation(out=y[:, t, :], in_=w[:], func=ACT.Identity, bias=bias[:, 4 * g + t : 4 * g + t + 1])
+        s1_banks = {}
+
+        def stage1_pass(h, g, t, o):
+            cols = slice((4 * g + t) * P, (4 * g + t + 1) * P)
+            if o == 0:
+                s1_banks[h, g, t] = bank()
+            nc.tensor.matmul_mx(
+                out=s1_banks[h, g, t][:],
+                lhsT=w_codes[o][:, cols].bitcast(FP8X4),
+                lhsT_scale=w_sc[4 * o : P, cols],
+                rhs=x_codes[o][h][:].bitcast(FP8X4),
+                rhs_scale=x_sc[o][h][:],
+                start=(o == 0),
+                stop=(o == 1),
+            )
+
+        def add_bias(h, g, t):
+            if (h, g) not in y_of:
+                y_of[h, g] = work.tile([P, 4, HALF], F32, name="y", tag="y", bufs=3)
+            w = s1_banks.pop((h, g, t))
+            nc.scalar.activation(
+                out=y_of[h, g][:, t, :], in_=w[:], func=ACT.Identity, bias=bias[:, 4 * g + t : 4 * g + t + 1]
+            )
+
+        def slices(h, g, t0, t1):
+            for t in range(t0, t1):
+                stage1_pass(h, g, t, 0)
+                stage1_pass(h, g, t, 1)
+                add_bias(h, g, t)
 
         def leaky(h, g):
             y = y_of.pop((h, g))
@@ -203,201 +219,287 @@ def tile_conditionalmixturelogisticcdfcouplingmap_d2p_kernel(
 
         st = {}
 
-        def stage2(j):
+        def stage2(name, j):
             h, jj = divmod(j, HALF_TILES)
             toks = slice(jj * P, (jj + 1) * P)
-            for name, grp in (("l", 2), ("mu", 1), ("pl", 0)):
-                w = bank()
-                st[name, j] = w
-                for k in range(K):
-                    cols = slice(grp * 512 + k * P, grp * 512 + (k + 1) * P)
-                    for g in range(PASSES2):
-                        nc.tensor.matmul_mx(
-                            out=w[:, k * P : (k + 1) * P],
-                            lhsT=wo_codes[g][:, cols].bitcast(FP8X4),
-                            lhsT_scale=wo_sc[4 * g : P, cols],
-                            rhs=h_codes[g][h][:, toks].bitcast(FP8X4),
-                            rhs_scale=h_sc[g][h][:, toks],
-                            start=(g == 0),
-                            stop=(g == PASSES2 - 1),
-                        )
+            grp = ("pl", "mu", "l").index(name)
+            w = bank()
+            st[name, j] = w
+            for k in range(K):
+                cols = slice(grp * 512 + k * P, grp * 512 + (k + 1) * P)
+                for g in range(PASSES2):
+                    nc.tensor.matmul_mx(
+                        out=w[:, k * P : (k + 1) * P],
+                        lhsT=wo_codes[g][:, cols].bitcast(FP8X4),
+                        lhsT_scale=wo_sc[4 * g : P, cols],
+                        rhs=h_codes[g][h][:, toks].bitcast(FP8X4),
+                        rhs_scale=h_sc[g][h][:, toks],
+                        start=(g == 0),
+                        stop=(g == PASSES2 - 1),
+                    )
 
-        def sb(name, j, bufs=4):
-            t = work.tile([P, K * DB], F32, name=name, tag=name, bufs=bufs)
-            st[name, j] = t
-            return t
+        depth = {"t": 3, "q": 4, "s": 3, "d": 3, "z": 3, "T": 4, "e": 4, "v": 3}
+
+        def tile_of(name, j):
+            if (name, j) not in st:
+                st[name, j] = work.tile([P, K * DB], F32, name=name, tag=name, bufs=depth[name])
+            return st[name, j][:]
+
+        def pair_of(name, p):
+            if (name, p) not in st:
+                st[name, p] = work.tile([P, 2, K * DB], F32, name=name, tag=name, bufs=depth[name])
+            return st[name, p]
+
+        def half_of(name, j):
+            return pair_of(name, j // 2)[:, j % 2, :]
 
         def a_tanh(j):
-            nc.scalar.activation(out=sb("t", j)[:], in_=st.pop(("l", j))[:], func=ACT.Tanh)
+            nc.scalar.activation(out=tile_of("t", j), in_=st.pop(("l", j))[:], func=ACT.Tanh)
 
         def a_exp(j):
-            nc.scalar.activation(out=sb("s", j)[:], in_=st.pop(("t", j))[:], func=ACT.Exp, scale=-1.0)
+            nc.scalar.activation(out=half_of("s", j), in_=tile_of("t", j), func=ACT.Exp, scale=-1.0)
 
         def v_diff(j):
             x3 = xb_t[:, j * P : (j + 1) * P].unsqueeze(1).to_broadcast([P, K, P])
             nc.vector.tensor_tensor(
-                out=sb("d", j)[:].rearrange("p (k n) -> p k n", k=K),
+                out=half_of("d", j).rearrange("p (k n) -> p k n", k=K),
                 in0=st.pop(("mu", j))[:].rearrange("p (k n) -> p k n", k=K),
                 in1=x3,
                 op=ALU.subtract,
             )
 
         def v_max(j):
-            m = work.tile([P, P], F32, name="m", tag="m", bufs=2)
+            m = work.tile([P, P], F32, name="m", tag="m", bufs=4)
             st["m", j] = m
             nc.vector.tensor_reduce(out=m[:], in_=st["pl", j][:].rearrange("p (k n) -> p n k", k=K), axis=AX.X, op=ALU.max)
 
         def v_sub(j):
             m3 = st.pop(("m", j))[:].unsqueeze(1).to_broadcast([P, K, P])
             nc.vector.tensor_tensor(
-                out=sb("q", j)[:].rearrange("p (k n) -> p k n", k=K),
+                out=tile_of("q", j).rearrange("p (k n) -> p k n", k=K),
                 in0=st.pop(("pl", j))[:].rearrange("p (k n) -> p k n", k=K),
                 in1=m3,
                 op=ALU.subtract,
             )
 
-        def v_z(j, eng):
-            eng.tensor_tensor(out=sb("z", j)[:], in0=st["d", j][:], in1=st.pop(("s", j))[:], op=ALU.mult)
-
         def a_e(j):
-            nc.scalar.activation(out=sb("e", j)[:], in_=st.pop(("q", j))[:], func=ACT.Exp)
+            nc.scalar.activation(out=half_of("e", j), in_=tile_of("q", j), func=ACT.Exp)
 
         def a_T(j):
-            nc.scalar.activation(out=sb("T", j)[:], in_=st.pop(("z", j))[:], func=ACT.Tanh, scale=-0.5)
+            nc.scalar.activation(out=half_of("T", j), in_=half_of("z", j), func=ACT.Tanh, scale=-0.5)
 
-        def v_eT(j, eng, into):
-            st["v", j] = st.pop(("d", into))
-            eng.tensor_tensor(out=st["v", j][:], in0=st["e", j][:], in1=st.pop(("T", j))[:], op=ALU.mult)
+        def mul_tile(out, a, b, j):
+            nc.vector.tensor_tensor(out=half_of(out, j), in0=half_of(a, j), in1=half_of(b, j), op=ALU.mult)
 
-        def sums(j):
-            if j % 2 == 0:
-                st["ev", j // 2] = psum.tile([P, 2, 2, P], F32, name="ev", tag="ev", bufs=2)
-            ev = st["ev", j // 2]
-            for i, name in enumerate(("e", "v")):
-                src = st.pop((name, j))
-                for k in range(K):
-                    nc.tensor.matmul(
-                        ev[:, j % 2, i, :],
-                        lhsT=src[:, k * P : (k + 1) * P],
-                        rhs=ident[:],
-                        is_transpose=True,
-                        start=(k == 0),
-                        stop=(k == K - 1),
-                    )
+        def mul_pair(out, a, b, p):
+            nc.gpsimd.tensor_tensor(out=pair_of(out, p)[:], in0=pair_of(a, p)[:], in1=pair_of(b, p)[:], op=ALU.mult)
 
-        def finish_pair(pr):
-            ev = st.pop(("ev", pr))
-            es = work.tile([P, 2, P], F32, name="es", tag="es", bufs=2)
-            cols = slice(2 * pr * P, (2 * pr + 2) * P)
-            if pr < 2:
-                nc.scalar.activation(out=es[:], in_=ev[:, :, 0, :], func=ACT.Copy, scale=1.0 / 0.98)
+        def product(out, a, b, j, on_gpsimd):
+            if j // 2 not in on_gpsimd:
+                mul_tile(out, a, b, j)
+            elif j % 2 == 1:
+                mul_pair(out, a, b, j // 2)
+
+        def sums(name, j):
+            if ("ev", j // 2) not in st:
+                if j < HALF_TILES:
+                    ev = psum.tile([P, 512], F32, name="ev", tag="ev", bufs=2)
+                else:
+                    ev = bank()
+                st["ev", j // 2] = ev[:].rearrange("p (j i d) -> p j i d", j=2, i=2)
+            src = half_of(name, j)
+            for k in range(K):
+                nc.tensor.matmul(
+                    st["ev", j // 2][:, j % 2, ("e", "v").index(name), :],
+                    lhsT=src[:, k * P : (k + 1) * P],
+                    rhs=ident[:],
+                    is_transpose=True,
+                    start=(k == 0),
+                    stop=(k == K - 1),
+                )
+
+        def copy_e(j0, j1, on_scalar):
+            n = j1 - j0
+            es = work.tile([P, 2, P], F32, name="es", tag="es", bufs=4)
+            st["es", j0] = es
+            src = st["ev", j0 // 2][:, j0 % 2 : j0 % 2 + n, 0, :]
+            if on_scalar:
+                nc.scalar.activation(out=es[:, 0:n, :], in_=src, func=ACT.Copy, scale=1.0 / 0.98)
             else:
-                nc.vector.tensor_scalar(out=es[:], in0=ev[:, :, 0, :], scalar1=1.0 / 0.98, scalar2=None, op0=ALU.mult)
-            a = ab[:, 0, cols].rearrange("p (j d) -> p j d", j=2)
-            bb = ab[:, 1, cols].rearrange("p (j d) -> p j d", j=2)
-            nc.vector.tensor_tensor(out=a, in0=ev[:, :, 1, :], in1=es[:], op=ALU.add)
-            nc.vector.tensor_tensor(out=bb, in0=es[:], in1=ev[:, :, 1, :], op=ALU.subtract)
+                nc.vector.tensor_scalar(out=es[:, 0:n, :], in0=src, scalar1=1.0 / 0.98, scalar2=None, op0=ALU.mult)
+
+        def ab_cols(i, j0, j1):
+            return ab[:, i, j0 * P : j1 * P].rearrange("p (j d) -> p j d", d=P)
+
+        def v_a(j0, j1):
+            n = j1 - j0
+            nc.vector.tensor_tensor(
+                out=ab_cols(0, j0, j1),
+                in0=st["ev", j0 // 2][:, j0 % 2 : j0 % 2 + n, 1, :],
+                in1=st["es", j0][:, 0:n, :],
+                op=ALU.add,
+            )
+
+        def v_b(j0, j1):
+            n = j1 - j0
+            nc.vector.tensor_tensor(
+                out=ab_cols(1, j0, j1),
+                in0=st["es", j0][:, 0:n, :],
+                in1=st["ev", j0 // 2][:, j0 % 2 : j0 % 2 + n, 1, :],
+                op=ALU.subtract,
+            )
 
         out_rows = out.rearrange("(j p) d -> p j d", p=P)
 
-        def logs(p0, p1):
-            cols = slice(2 * p0 * P, 2 * p1 * P)
+        def logs(j0, j1):
+            cols = slice(j0 * P, j1 * P)
             nc.scalar.activation(out=ln_ab[:, :, cols], in_=ab[:, :, cols], func=ACT.Ln)
 
-        def write_out(p0, p1):
-            cols = slice(2 * p0 * P, 2 * p1 * P)
+        def write_out(j0, j1):
+            cols = slice(j0 * P, j1 * P)
             nc.vector.tensor_tensor(out=out_sb[:, cols], in0=ln_ab[:, 0, cols], in1=ln_ab[:, 1, cols], op=ALU.subtract)
-            nc.sync.dma_start(
-                out=out_rows[:, 2 * p0 : 2 * p1, :], in_=out_sb[:, cols].rearrange("p (j d) -> p j d", d=DB)
-            )
+            nc.sync.dma_start(out=out_rows[:, j0:j1, :], in_=out_sb[:, cols].rearrange("p (j d) -> p j d", d=DB))
 
-        def prep_xa(h):
-            new_in(("xa", h))
-            for pair in range(2):
-                empty_xa(h, pair, turn(xa_bf[h], pair), pair == 1)
+        def grouped_in(name, h):
+            if (name, h) not in x_in:
+                new_in((name, h))
+
+        banks_of = {}
+
+        def turn_xa(h, pair):
+            banks_of["xa", h, pair] = turn(xa_bf[h], pair)
+
+        def turn_c(h, pair):
+            banks_of["c", h, pair] = turn(c_sb[h], pair)
+
+        def out_xa(h, pair, on_scalar):
+            grouped_in("xa", h)
+            empty_xa(h, pair, banks_of.pop(("xa", h, pair)), on_scalar)
+
+        def out_c(h, pair):
+            grouped_in("c", h)
+            empty_c(h, pair, banks_of.pop(("c", h, pair)))
+
+        def turn_xb():
+            wx = bank(BF16, 1024)
+            banks_of["xb"] = wx
+            for j in range(TILES):
+                nc.tensor.transpose(wx[:, j * P : (j + 1) * P], xb_sb[:, j, :], ident_bf[:])
+
+        def out_xb():
+            nc.scalar.copy(out=xb_t[:], in_=banks_of.pop("xb")[:])
 
         def quant_xa(h):
             quantize(x_in.pop(("xa", h)), x_codes[0][h], x_sc[0][h])
-
-        def prep_c(h):
-            new_in(("c", h))
-            for pair in range(2):
-                empty_c(h, pair, turn(c_sb[h], pair))
 
         def quant_c(h):
             quantize(x_in.pop(("c", h)), x_codes[1][h], x_sc[1][h])
 
         cast_xa(0, "v", 0, 2)
         cast_xa(0, "s", 2, 4)
-        prep_xa(0)
-        prep_c(0)
+        for pair in range(2):
+            turn_xa(0, pair)
+        for pair in range(2):
+            turn_c(0, pair)
         permute(0, 0)
-        quant_xa(0)
+        out_xa(0, 0, False)
+        out_xa(0, 1, True)
         permute_scales(0)
+        quant_xa(0)
+        out_c(0, 1)
         permute(1, 0)
-        quant_c(0)
-        permute(0, 1)
+        out_c(0, 0)
         permute(1, 1)
-        permute_scales(1)
-        stage1(0, 0)
+        quant_c(0)
+        for t in range(4):
+            stage1_pass(0, 0, t, 0)
         cast_xa(1, "v", 0, 2)
         cast_xa(1, "s", 2, 4)
-        stage1(0, 1)
+        for t in range(4):
+            stage1_pass(0, 0, t, 1)
+            add_bias(0, 0, t)
+        permute_scales(1)
+        permute(0, 1)
+        slices(0, 1, 0, 0)
+        for pair in range(2):
+            turn_xa(1, pair)
+        out_xa(1, 0, False)
+        out_xa(1, 1, True)
         leaky(0, 0)
-        prep_xa(1)
-        quantize_h(0, 0)
-        prep_c(1)
+        slices(0, 1, 0, 2)
         quant_xa(1)
+        for pair in range(2):
+            turn_c(1, pair)
+            out_c(1, pair)
         quant_c(1)
+        quantize_h(0, 0)
+        slices(0, 1, 2, 4)
         leaky(0, 1)
-        wx = bank(BF16, 1024)
-        for j in range(TILES):
-            nc.tensor.transpose(wx[:, j * P : (j + 1) * P], xb_sb[:, j, :], ident_bf[:])
-        nc.scalar.copy(out=xb_t[:], in_=wx[:])
+        turn_xb()
+        out_xb()
+        slices(1, 0, 0, 4)
         quantize_h(0, 1)
-        stage1(1, 0)
         leaky(1, 0)
-        stage1(1, 1)
-        stage2(0)
-        a_tanh(0)
-        a_exp(0)
-        v_max(0)
-        quantize_h(1, 0)
+        slices(1, 1, 0, 4)
         leaky(1, 1)
-        v_diff(0)
-        v_sub(0)
+        quantize_h(1, 0)
         quantize_h(1, 1)
-        v_z(0, nc.vector)
-        stage2(1)
-        a_tanh(1)
-        a_exp(1)
-        for i in range(1, TILES):
-            if i + 1 < TILES:
-                stage2(i + 1)
-            v_max(i)
-            v_diff(i)
-            a_e(i - 1)
-            v_sub(i)
-            a_T(i - 1)
-            v_z(i, nc.vector)
-            if i + 1 < TILES:
-                a_tanh(i + 1)
-                a_exp(i + 1)
-            v_eT(i - 1, nc.gpsimd if i < TILES - 1 else nc.vector, i)
-            if i >= 3 and i % 2 == 1:
-                sums(i - 3)
-                sums(i - 2)
-            if i >= 4 and i % 2 == 0:
-                finish_pair((i - 4) // 2)
+        for j in range(TILES + 2):
+            if j < TILES:
+                stage2("l", j)
+                a_tanh(j)
+                a_exp(j)
+            if 1 <= j <= TILES:
+                stage2("mu", j - 1)
+                v_diff(j - 1)
+            if j >= 2:
+                product("z", "d", "s", j - 2, Z_ON_GPSIMD)
+        for j in range(TILES):
+            stage2("pl", j)
+            v_max(j)
+            if j >= 1:
+                v_sub(j - 1)
+            a_T(j)
+            if j >= 2:
+                a_e(j - 2)
+            if j >= 4:
+                sums("e", j - 4)
+            if 3 <= j < 7:
+                product("v", "e", "T", j - 3, V_ON_GPSIMD)
+        v_sub(TILES - 1)
+        a_e(TILES - 2)
+        for j in (4, 5):
+            sums("e", j)
         a_e(TILES - 1)
-        a_T(TILES - 1)
+        copy_e(0, 2, True)
+        for j in (0, 1):
+            sums("v", j)
+        mul_tile("v", "e", "T", 4)
+        mul_tile("v", "e", "T", 5)
+        v_a(0, 2)
+        v_b(0, 2)
+        copy_e(2, 4, True)
         nc.scalar.activation(out=warm[:], in_=warm[:], func=ACT.Ln)
-        sums(TILES - 2)
-        finish_pair(2)
-        v_eT(TILES - 1, nc.vector, 0)
-        sums(TILES - 1)
-        logs(0, 3)
-        finish_pair(3)
-        logs(3, 4)
-        write_out(0, 3)
-        write_out(3, 4)
+        for j in (6, 7):
+            sums("e", j)
+        for j in (2, 3):
+            sums("v", j)
+        mul_tile("v", "e", "T", 6)
+        copy_e(4, 6, False)
+        mul_tile("v", "e", "T", 7)
+        v_a(2, 4)
+        v_b(2, 4)
+        logs(0, 4)
+        for j in (4, 5):
+            sums("v", j)
+        copy_e(6, 8, False)
+        v_a(4, 6)
+        v_b(4, 6)
+        logs(4, 6)
+        for j in (6, 7):
+            sums("v", j)
+        v_a(6, 8)
+        v_b(6, 8)
+        logs(6, 8)
+        write_out(0, 6)
+        write_out(6, 8)

@@ -14,16 +14,20 @@ ALU = mybir.AluOpType
 AX = mybir.AxisListType
 
 P = 128
+PACK = 4
+GROUP = P * PACK
 TOKENS, D_IN, F, DB, K = 1024, 512, 1024, 128, 4
 J = 3 * K * DB
-HALF = 512
+GROUPS = F // GROUP
 TILES = TOKENS // P
-HALF_TILES = HALF // P
-PASSES2 = F // 512
+HALF_TILES = 4
+HALF = HALF_TILES * P
+PART = {"pl": 0, "mu": 1, "l": 2}
+SHRINK = 0.98
 
-Z_ON_GPSIMD = (2, 3)
-V_ON_GPSIMD = (0, 1)
-C_ON_VECTOR = ((0, 0),)
+Z_PAIRS_ON_GPSIMD = (2, 3)
+V_PAIRS_ON_GPSIMD = (0, 1)
+
 FLOPS = 2 * TOKENS * (2 * D_IN * F + F * J)
 
 
@@ -33,473 +37,440 @@ def tile_conditionalmixturelogisticcdfcouplingmap_d2p_kernel(
     nc = tc.nc
     with ExitStack() as ctx:
         keep = ctx.enter_context(tc.tile_pool(name="keep", bufs=1))
-        work = ctx.enter_context(tc.tile_pool(name="work", bufs=2))
+        work = ctx.enter_context(tc.tile_pool(name="work", bufs=1))
         psum = ctx.enter_context(tc.psum_pool(name="psum", bufs=1))
         ctx.enter_context(tc.manual_schedule())
 
+        def kept(name, cols, dtype):
+            tile = keep.tile([P, cols], dtype, name=name, align_bytes=64)
+            return tile
+
+        def kept_twice(name, cols, dtype):
+            return [kept(name + str(i), cols, dtype) for i in range(2)]
+
         def bank(dtype=F32, cols=512):
-            w = psum.tile([P, cols], dtype, name="w", tag="w", bufs=6)
-            return w
+            tile = psum.tile([P, cols], dtype, name="ring", tag="ring", bufs=6)
+            return tile
 
-        xa_u8 = [keep.tile([P, HALF_TILES * D_IN], U8, name="xa_u8_" + str(h), align_bytes=64) for h in range(2)]
-        c_sb = [keep.tile([P, HALF_TILES * D_IN], BF16, name="c_sb_" + str(h), align_bytes=64) for h in range(2)]
-        xa_bf = [keep.tile([P, HALF_TILES * D_IN], BF16, name="xa_bf_" + str(h), align_bytes=64) for h in range(2)]
-        xb_sb = keep.tile([P, TILES, DB], BF16, name="xb_sb", align_bytes=64)
-        xb_t = keep.tile([P, TOKENS], BF16, name="xb_t", align_bytes=64)
-        w_raw = [keep.tile([P, F], I32, name="w_raw_" + str(o), align_bytes=64) for o in range(2)]
-        w_codes = [keep.tile([P, F], I32, name="w_codes_" + str(o), align_bytes=64) for o in range(2)]
-        w_sc_raw = keep.tile([P, F], U8, name="w_sc_raw", align_bytes=64)
-        w_sc = keep.tile([P, F], U8, name="w_sc", align_bytes=64)
-        wo_codes = [keep.tile([P, J], I32, name="wo_codes_" + str(g), align_bytes=64) for g in range(2)]
-        wo_sc = keep.tile([P, J], U8, name="wo_sc", align_bytes=64)
-        x_codes = [[keep.tile([P, HALF], I32, name="x_codes_" + str(o) + str(h), align_bytes=64) for h in range(2)] for o in range(2)]
-        x_sc = [[keep.tile([P, HALF], U8, name="x_sc_" + str(o) + str(h), align_bytes=64) for h in range(2)] for o in range(2)]
-        h_codes = [[keep.tile([P, HALF], I32, name="h_codes_" + str(g) + str(h), align_bytes=64) for h in range(2)] for g in range(2)]
-        h_sc = [[keep.tile([P, HALF], U8, name="h_sc_" + str(g) + str(h), align_bytes=64) for h in range(2)] for g in range(2)]
-        sc_all = keep.tile([P, 32], F32, name="sc_all")
-        sc_col = keep.tile([P, TILES], F32, name="sc_col")
-        bias_bf = keep.tile([P, PASSES2, 4], BF16, name="bias_bf")
-        bias = keep.tile([P, PASSES2 * 4], F32, name="bias")
-        ident = keep.tile([P, P], F32, name="ident")
-        ident_bf = keep.tile([P, P], BF16, name="ident_bf")
-        ab = keep.tile([P, 2, TOKENS], F32, name="ab")
-        ln_ab = keep.tile([P, 2, TOKENS], F32, name="ln_ab")
-        out_sb = keep.tile([P, TOKENS], F32, name="out_sb")
-        warm = keep.tile([P, 1], F32, name="warm")
+        xa_u8 = kept_twice("xa_u8", HALF_TILES * D_IN, U8)
+        xa_bf = kept_twice("xa_bf", HALF_TILES * D_IN, BF16)
+        c_bf = kept_twice("c_bf", HALF_TILES * D_IN, BF16)
+        xa_scales = kept("xa_scales", TILES * (D_IN // P), F32)
+        xb_rows = kept("xb_rows", TILES * DB, BF16)
+        xb_turned = kept("xb_turned", TOKENS, BF16)
+        w_raw = kept_twice("w_raw", F, I32)
+        w_codes = kept_twice("w_codes", F, I32)
+        w_scales_raw = kept("w_scales_raw", F, U8)
+        w_scales = kept("w_scales", F, U8)
+        wo_codes = kept_twice("wo_codes", J, I32)
+        wo_scale_rows = kept("wo_scale_rows", J, U8)
+        x_codes = [kept_twice(name + "_codes", HALF, I32) for name in ("xa", "c")]
+        x_scale_rows = [kept_twice(name + "_scale_rows", HALF, U8) for name in ("xa", "c")]
+        h_codes = [kept_twice("h_codes_g" + str(g), HALF, I32) for g in range(GROUPS)]
+        h_scale_rows = [kept_twice("h_scale_rows_g" + str(g), HALF, U8) for g in range(GROUPS)]
+        bias_bf = kept("bias_bf", GROUPS * PACK, BF16)
+        bias = kept("bias", GROUPS * PACK, F32)
+        ident = kept("ident", P, F32)
+        ident_bf = kept("ident_bf", P, BF16)
+        ratio = keep.tile([P, 2, TOKENS], F32, name="ratio")
+        logs = keep.tile([P, 2, TOKENS], F32, name="logs")
+        result = kept("result", TOKENS, F32)
+        table_probe = kept("table_probe", 1, F32)
 
-        xa_rows = xa_bytes.rearrange("(j p) k -> p j k", p=P)
-        c_rows = c.rearrange("(j p) k -> p j k", p=P)
-
-        def load_xa(h):
-            tiles = slice(h * HALF_TILES, (h + 1) * HALF_TILES)
-            nc.sync.dma_start(out=xa_u8[h][:].rearrange("p (j k) -> p j k", k=D_IN), in_=xa_rows[:, tiles, :])
-
-        def load_c(h):
-            tiles = slice(h * HALF_TILES, (h + 1) * HALF_TILES)
-            nc.sync.dma_start(out=c_sb[h][:].rearrange("p (j k) -> p j k", k=D_IN), in_=c_rows[:, tiles, :])
+        def load_rows(tile, rows, h):
+            source = rows.rearrange("(j p) k -> p j k", p=P)[:, h * HALF_TILES : (h + 1) * HALF_TILES, :]
+            nc.sync.dma_start(out=tile[:].rearrange("p (j k) -> p j k", k=D_IN), in_=source)
 
         def load_words(tile, words):
             nc.sync.dma_start(out=tile[:], in_=words.rearrange("p n t -> p (n t)").bitcast(I32))
 
-        def load_scales(queue, tile, scales, first, q):
+        def load_scale_rows(queue, tile, scales, first, q):
             rows = slice(32 * q + first, 32 * q + first + 4)
             queue.dma_start(out=tile[rows, :].bitcast(I32), in_=scales[4 * q : 4 * q + 4, :].bitcast(I32))
 
-        nc.vector.memset(w_sc_raw[:].bitcast(I32), 0)
-        nc.vector.memset(wo_sc[:].bitcast(I32), 0)
-        nc.vector.memset(warm[:], 1.0)
+        nc.vector.memset(w_scales_raw[:].bitcast(I32), 0)
+        nc.vector.memset(wo_scale_rows[:].bitcast(I32), 0)
+        nc.vector.memset(table_probe[:], 1.0)
         make_identity(nc, ident[:])
-        nc.scalar.dma_start(out=sc_all[:], in_=xa_scale.rearrange("i j -> (i j)").partition_broadcast(P))
-        nc.scalar.dma_start(out=bias_bf[:], in_=b.rearrange("(g p t) -> p g t", p=P, t=4))
+
+        nc.scalar.dma_start(out=xa_scales[:], in_=xa_scale.rearrange("i j -> (i j)").partition_broadcast(P))
+        nc.scalar.dma_start(
+            out=bias_bf[:].rearrange("p (g t) -> p g t", t=PACK), in_=b.rearrange("(g p t) -> p g t", p=P, t=PACK)
+        )
         for q in range(3):
-            load_scales(nc.scalar, w_sc_raw, wa_scales[0], 0, q)
-        load_xa(0)
-        load_c(0)
+            load_scale_rows(nc.scalar, w_scales_raw, wa_scales[0], 0, q)
+        load_rows(xa_u8[0], xa_bytes, 0)
+        load_rows(c_bf[0], c, 0)
         load_words(w_raw[0], wa_words[0])
-        nc.scalar.activation(out=warm[:], in_=warm[:], func=ACT.Exp)
-        load_scales(nc.sync, w_sc_raw, wa_scales[0], 0, 3)
+        nc.scalar.activation(out=table_probe[:], in_=table_probe[:], func=ACT.Exp)
+        load_scale_rows(nc.sync, w_scales_raw, wa_scales[0], 0, 3)
         for q in range(4):
-            load_scales(nc.sync, w_sc_raw, wc_scales[0], 4, q)
+            load_scale_rows(nc.sync, w_scales_raw, wc_scales[0], 4, q)
         load_words(w_raw[1], wc_words[0])
-        load_xa(1)
-        load_c(1)
-        nc.sync.dma_start(out=xb_sb[:], in_=xb.rearrange("(j p) d -> p j d", p=P))
-        for g in range(PASSES2):
+        load_rows(xa_u8[1], xa_bytes, 1)
+        load_rows(c_bf[1], c, 1)
+        nc.sync.dma_start(out=xb_rows[:].rearrange("p (j d) -> p j d", d=DB), in_=xb.rearrange("(j p) d -> p j d", p=P))
+        for g in range(GROUPS):
             load_words(wo_codes[g], wo_words[g])
-        for g in range(PASSES2):
+        for g in range(GROUPS):
             for q in range(4):
-                load_scales(nc.sync, wo_sc, wo_scales[g], 4 * g, q)
+                load_scale_rows(nc.sync, wo_scale_rows, wo_scales[g], 4 * g, q)
         nc.vector.tensor_copy(out=ident_bf[:], in_=ident[:])
-        for q in range(4):
-            nc.vector.tensor_copy(out=sc_col[32 * q : 32 * q + 32, :], in_=sc_all[32 * q : 32 * q + 32, q::4])
-        nc.vector.tensor_copy(out=bias[:], in_=bias_bf[:].rearrange("p g t -> p (g t)"))
+        nc.vector.tensor_copy(out=bias[:], in_=bias_bf[:])
 
-        def cast_xa(h, eng, t0, t1):
-            cols = slice(t0 * D_IN, t1 * D_IN)
-            src = xa_u8[h][:, cols].bitcast(FP8)
-            if eng == "v":
-                nc.vector.tensor_copy(out=xa_bf[h][:, cols], in_=src)
-            else:
-                nc.scalar.copy(out=xa_bf[h][:, cols], in_=src)
+        def scale_xa(h, on_scalar, j0, j1):
+            for j in range(j0, j1):
+                for block in range(D_IN // P):
+                    cols = slice(j * D_IN + block * P, j * D_IN + (block + 1) * P)
+                    s = (h * HALF_TILES + j) * (D_IN // P) + block
+                    values = xa_u8[h][:, cols].bitcast(FP8)
+                    factor = xa_scales[:, s : s + 1]
+                    if on_scalar:
+                        nc.scalar.activation(out=xa_bf[h][:, cols], in_=values, func=ACT.Copy, scale=factor)
+                    else:
+                        nc.vector.tensor_scalar(
+                            out=xa_bf[h][:, cols], in0=values, scalar1=factor, scalar2=None, op0=ALU.mult
+                        )
 
-        def turn(src, pair):
+        turned = {}
+
+        def turn(name, source, h, pair):
             w = bank()
-            words = src[:].bitcast(F32)
+            words = source[h][:].bitcast(F32)
             for jj in range(2):
                 for u in range(2):
-                    base = (2 * pair + jj) * (D_IN // 2)
+                    first = (2 * pair + jj) * (D_IN // 2)
                     nc.tensor.transpose(
-                        w[:, (2 * jj + u) * P : (2 * jj + u + 1) * P], words[:, base + u : base + D_IN // 2 : 2], ident[:]
+                        w[:, (2 * jj + u) * P : (2 * jj + u + 1) * P], words[:, first + u : first + D_IN // 2 : 2], ident[:]
                     )
-            return w
+            turned[name, h, pair] = w
 
-        x_in = {}
+        grouped = {}
 
-        def new_in(name):
-            x_in[name] = work.tile([P, 4 * HALF], BF16, name="grouped", tag="grouped", bufs=4, align_bytes=64)
-            return x_in[name]
+        def grouped_tile(key):
+            if key not in grouped:
+                grouped[key] = work.tile([P, PACK * HALF], BF16, name="grouped", tag="grouped", bufs=4, align_bytes=64)
+            return grouped[key]
 
-        def empty_xa(h, pair, w, on_scalar):
-            for jj in range(2):
-                j = 2 * pair + jj
-                src = w[:, 2 * jj * P : (2 * jj + 2) * P].bitcast(BF16).rearrange("p (u n e) -> p n u e", u=2, e=2)
-                dst = x_in["xa", h][:, j * D_IN : (j + 1) * D_IN].rearrange("p (n u e) -> p n u e", u=2, e=2)
-                jt = h * HALF_TILES + j
-                if on_scalar:
-                    nc.scalar.activation(out=dst, in_=src, func=ACT.Copy, scale=sc_col[:, jt : jt + 1])
-                else:
-                    nc.vector.tensor_scalar(out=dst, in0=src, scalar1=sc_col[:, jt : jt + 1], scalar2=None, op0=ALU.mult)
-
-        def empty_c(h, pair, w):
-            dst = x_in["c", h][:, 2 * pair * D_IN : (2 * pair + 2) * D_IN].bitcast(F32)
-            dst = dst.rearrange("p (j n u) -> p j n u", j=2, u=2)
-            src = w[:].rearrange("p (j u n) -> p j n u", j=2, u=2)
-            if (h, pair) in C_ON_VECTOR:
-                nc.vector.tensor_copy(out=dst, in_=src)
-            else:
+        def interleave(name, h, pair, on_scalar):
+            tile = grouped_tile((name, h))[:, 2 * pair * D_IN : (2 * pair + 2) * D_IN].bitcast(F32)
+            dst = tile.rearrange("p (j n u) -> p j n u", j=2, u=2)
+            src = turned.pop((name, h, pair))[:].rearrange("p (j u n) -> p j n u", j=2, u=2)
+            if on_scalar:
                 nc.scalar.copy(out=dst, in_=src)
+            else:
+                nc.vector.tensor_copy(out=dst, in_=src)
 
-        def quantize(src, codes, scales):
-            nc.vector.quantize_mx(out=codes[:].bitcast(FP8X4), scales=scales[:], in_=src[:])
+        def quantize(key, codes, scale_rows):
+            source = grouped.pop(key)
+            nc.vector.quantize_mx(out=codes[:].bitcast(FP8X4), scales=scale_rows[:], in_=source[:])
 
-        def permute(o, g):
-            cols = slice(512 * g, 512 * g + 512)
+        def quantize_x(o, h):
+            quantize((("xa", "c")[o], h), x_codes[o][h], x_scale_rows[o][h])
+
+        def quantize_h(h, g):
+            quantize(("h", g, h), h_codes[g][h], h_scale_rows[g][h])
+
+        def reorder(dst, src, g):
+            cols = slice(GROUP * g, GROUP * (g + 1))
             nc.vector.tensor_copy(
-                out=w_codes[o][:, cols].rearrange("p (t m) -> p t m", t=4), in_=w_raw[o][:, cols].rearrange("p (m t) -> p t m", t=4)
+                out=dst[:, cols].rearrange("p (t m) -> p t m", t=PACK), in_=src[:, cols].rearrange("p (m t) -> p t m", t=PACK)
             )
 
-        def permute_scales(g):
-            cols = slice(512 * g, 512 * g + 512)
-            nc.vector.tensor_copy(
-                out=w_sc[:, cols].rearrange("p (t m) -> p t m", t=4), in_=w_sc_raw[:, cols].rearrange("p (m t) -> p t m", t=4)
-            )
-
-        y_of = {}
-
-        s1_banks = {}
+        stage1_banks = {}
+        y_tiles = {}
 
         def stage1_pass(h, g, t, o):
-            cols = slice((4 * g + t) * P, (4 * g + t + 1) * P)
+            cols = slice((PACK * g + t) * P, (PACK * g + t + 1) * P)
             if o == 0:
-                s1_banks[h, g, t] = bank()
+                stage1_banks[h, g, t] = bank()
             nc.tensor.matmul_mx(
-                out=s1_banks[h, g, t][:],
+                out=stage1_banks[h, g, t][:],
                 lhsT=w_codes[o][:, cols].bitcast(FP8X4),
-                lhsT_scale=w_sc[4 * o : P, cols],
+                lhsT_scale=w_scales[4 * o : P, cols],
                 rhs=x_codes[o][h][:].bitcast(FP8X4),
-                rhs_scale=x_sc[o][h][:],
+                rhs_scale=x_scale_rows[o][h][:],
                 start=(o == 0),
                 stop=(o == 1),
             )
 
         def add_bias(h, g, t):
-            if (h, g) not in y_of:
-                y_of[h, g] = work.tile([P, 4, HALF], F32, name="y", tag="y", bufs=3)
-            w = s1_banks.pop((h, g, t))
+            if (h, g) not in y_tiles:
+                y_tiles[h, g] = work.tile([P, PACK, HALF], F32, name="y", tag="y", bufs=3)
             nc.scalar.activation(
-                out=y_of[h, g][:, t, :], in_=w[:], func=ACT.Identity, bias=bias[:, 4 * g + t : 4 * g + t + 1]
+                out=y_tiles[h, g][:, t, :],
+                in_=stage1_banks.pop((h, g, t))[:],
+                func=ACT.Identity,
+                bias=bias[:, PACK * g + t : PACK * g + t + 1],
             )
 
-        def slices(h, g, t0, t1):
+        def stage1_slices(h, g, t0, t1):
             for t in range(t0, t1):
                 stage1_pass(h, g, t, 0)
                 stage1_pass(h, g, t, 1)
                 add_bias(h, g, t)
 
         def leaky(h, g):
-            y = y_of.pop((h, g))
-            grouped = new_in(("h", g, h))
-            yv = y[:].rearrange("p t n -> p n t")
-            nc.vector.scalar_tensor_tensor(
-                out=grouped[:].rearrange("p (n t) -> p n t", t=4), in0=yv, scalar=0.2, in1=yv, op0=ALU.mult, op1=ALU.max
-            )
+            y = y_tiles.pop((h, g))[:].rearrange("p t n -> p n t")
+            dst = grouped_tile(("h", g, h))[:].rearrange("p (n t) -> p n t", t=PACK)
+            nc.vector.scalar_tensor_tensor(out=dst, in0=y, scalar=0.2, in1=y, op0=ALU.mult, op1=ALU.max)
 
-        def quantize_h(h, g):
-            quantize(x_in.pop(("h", g, h)), h_codes[g][h], h_sc[g][h])
-
-        st = {}
+        banks = {}
 
         def stage2(name, j):
             h, jj = divmod(j, HALF_TILES)
-            toks = slice(jj * P, (jj + 1) * P)
-            grp = ("pl", "mu", "l").index(name)
+            tokens = slice(jj * P, (jj + 1) * P)
             w = bank()
-            st[name, j] = w
+            banks[name, j] = w
             for k in range(K):
-                cols = slice(grp * 512 + k * P, grp * 512 + (k + 1) * P)
-                for g in range(PASSES2):
+                first = (PART[name] * K + k) * DB
+                cols = slice(first, first + DB)
+                for g in range(GROUPS):
                     nc.tensor.matmul_mx(
                         out=w[:, k * P : (k + 1) * P],
                         lhsT=wo_codes[g][:, cols].bitcast(FP8X4),
-                        lhsT_scale=wo_sc[4 * g : P, cols],
-                        rhs=h_codes[g][h][:, toks].bitcast(FP8X4),
-                        rhs_scale=h_sc[g][h][:, toks],
+                        lhsT_scale=wo_scale_rows[4 * g : P, cols],
+                        rhs=h_codes[g][h][:, tokens].bitcast(FP8X4),
+                        rhs_scale=h_scale_rows[g][h][:, tokens],
                         start=(g == 0),
-                        stop=(g == PASSES2 - 1),
+                        stop=(g == GROUPS - 1),
                     )
 
-        depth = {"t": 3, "q": 4, "s": 3, "d": 3, "z": 3, "T": 4, "e": 4, "v": 3}
+        def by_component(ap):
+            return ap.rearrange("p (k n) -> p k n", k=K)
+
+        def over_components(ap):
+            return ap.unsqueeze(1).to_broadcast([P, K, P])
+
+        depth = {"t": 3, "q": 4, "s": 3, "diff": 3, "z": 3, "T": 4, "e": 4, "v": 3}
+        tiles = {}
 
         def tile_of(name, j):
-            if (name, j) not in st:
-                st[name, j] = work.tile([P, K * DB], F32, name=name, tag=name, bufs=depth[name])
-            return st[name, j][:]
+            if (name, j) not in tiles:
+                tiles[name, j] = work.tile([P, K * P], F32, name=name, tag=name, bufs=depth[name])
+            return tiles[name, j][:]
 
-        def pair_of(name, p):
-            if (name, p) not in st:
-                st[name, p] = work.tile([P, 2, K * DB], F32, name=name, tag=name, bufs=depth[name])
-            return st[name, p]
+        def pair_of(name, pair):
+            if (name, pair) not in tiles:
+                tiles[name, pair] = work.tile([P, 2, K * P], F32, name=name, tag=name, bufs=depth[name])
+            return tiles[name, pair]
 
         def half_of(name, j):
             return pair_of(name, j // 2)[:, j % 2, :]
 
-        def a_tanh(j):
-            nc.scalar.activation(out=tile_of("t", j), in_=st.pop(("l", j))[:], func=ACT.Tanh)
+        def tanh_l(j):
+            nc.scalar.activation(out=tile_of("t", j), in_=banks.pop(("l", j))[:], func=ACT.Tanh)
 
-        def a_exp(j):
+        def exp_scale(j):
             nc.scalar.activation(out=half_of("s", j), in_=tile_of("t", j), func=ACT.Exp, scale=-1.0)
 
-        def v_diff(j):
-            x3 = xb_t[:, j * P : (j + 1) * P].unsqueeze(1).to_broadcast([P, K, P])
+        def difference(j):
             nc.vector.tensor_tensor(
-                out=half_of("d", j).rearrange("p (k n) -> p k n", k=K),
-                in0=st.pop(("mu", j))[:].rearrange("p (k n) -> p k n", k=K),
-                in1=x3,
+                out=by_component(half_of("diff", j)),
+                in0=by_component(banks.pop(("mu", j))[:]),
+                in1=over_components(xb_turned[:, j * P : (j + 1) * P]),
                 op=ALU.subtract,
             )
 
-        def v_max(j):
-            m = work.tile([P, P], F32, name="m", tag="m", bufs=4)
-            st["m", j] = m
-            nc.vector.tensor_reduce(out=m[:], in_=st["pl", j][:].rearrange("p (k n) -> p n k", k=K), axis=AX.X, op=ALU.max)
+        def maximum(j):
+            tiles["max", j] = work.tile([P, P], F32, name="max", tag="max", bufs=4)
+            nc.vector.tensor_reduce(
+                out=tiles["max", j][:],
+                in_=banks["pl", j][:].rearrange("p (k n) -> p n k", k=K),
+                axis=AX.X,
+                op=ALU.max,
+            )
 
-        def v_sub(j):
-            m3 = st.pop(("m", j))[:].unsqueeze(1).to_broadcast([P, K, P])
+        def subtract_maximum(j):
             nc.vector.tensor_tensor(
-                out=tile_of("q", j).rearrange("p (k n) -> p k n", k=K),
-                in0=st.pop(("pl", j))[:].rearrange("p (k n) -> p k n", k=K),
-                in1=m3,
+                out=by_component(tile_of("q", j)),
+                in0=by_component(banks.pop(("pl", j))[:]),
+                in1=over_components(tiles.pop(("max", j))[:]),
                 op=ALU.subtract,
             )
 
-        def a_e(j):
+        def exp_e(j):
             nc.scalar.activation(out=half_of("e", j), in_=tile_of("q", j), func=ACT.Exp)
 
-        def a_T(j):
+        def tanh_z(j):
             nc.scalar.activation(out=half_of("T", j), in_=half_of("z", j), func=ACT.Tanh, scale=-0.5)
 
-        def mul_tile(out, a, b, j):
-            nc.vector.tensor_tensor(out=half_of(out, j), in0=half_of(a, j), in1=half_of(b, j), op=ALU.mult)
-
-        def mul_pair(out, a, b, p):
-            nc.gpsimd.tensor_tensor(out=pair_of(out, p)[:], in0=pair_of(a, p)[:], in1=pair_of(b, p)[:], op=ALU.mult)
-
-        def product(out, a, b, j, on_gpsimd):
-            if j // 2 not in on_gpsimd:
-                mul_tile(out, a, b, j)
+        def product(result_name, a, b_name, j, pairs_on_gpsimd):
+            if j // 2 not in pairs_on_gpsimd:
+                nc.vector.tensor_tensor(
+                    out=half_of(result_name, j), in0=half_of(a, j), in1=half_of(b_name, j), op=ALU.mult
+                )
             elif j % 2 == 1:
-                mul_pair(out, a, b, j // 2)
+                nc.gpsimd.tensor_tensor(
+                    out=pair_of(result_name, j // 2)[:],
+                    in0=pair_of(a, j // 2)[:],
+                    in1=pair_of(b_name, j // 2)[:],
+                    op=ALU.mult,
+                )
 
-        def sums(name, j):
-            if ("ev", j // 2) not in st:
+        def product_z(j):
+            product("z", "diff", "s", j, Z_PAIRS_ON_GPSIMD)
+
+        def product_v(j):
+            product("v", "e", "T", j, V_PAIRS_ON_GPSIMD)
+
+        sums_banks = {}
+
+        def sum_components(name, j):
+            pair = j // 2
+            if pair not in sums_banks:
                 if j < HALF_TILES:
-                    ev = psum.tile([P, 512], F32, name="ev", tag="ev", bufs=2)
+                    sums_banks[pair] = psum.tile([P, 512], F32, name="sums", tag="sums", bufs=2)
                 else:
-                    ev = bank()
-                st["ev", j // 2] = ev[:].rearrange("p (j i d) -> p j i d", j=2, i=2)
-            src = half_of(name, j)
+                    sums_banks[pair] = bank()
+            first = (2 * (j % 2) + ("e", "v").index(name)) * P
             for k in range(K):
                 nc.tensor.matmul(
-                    st["ev", j // 2][:, j % 2, ("e", "v").index(name), :],
-                    lhsT=src[:, k * P : (k + 1) * P],
+                    sums_banks[pair][:, first : first + P],
+                    lhsT=half_of(name, j)[:, k * P : (k + 1) * P],
                     rhs=ident[:],
                     is_transpose=True,
                     start=(k == 0),
                     stop=(k == K - 1),
                 )
 
-        def copy_e(j0, j1, on_scalar):
-            n = j1 - j0
-            es = work.tile([P, 2, P], F32, name="es", tag="es", bufs=4)
-            st["es", j0] = es
-            src = st["ev", j0 // 2][:, j0 % 2 : j0 % 2 + n, 0, :]
+        def sums_of(pair, i):
+            return sums_banks[pair][:].rearrange("p (j i d) -> p j i d", j=2, i=2)[:, :, i, :]
+
+        def ratio_part(i, pair):
+            return ratio[:, i, 2 * pair * P : (2 * pair + 2) * P].rearrange("p (j d) -> p j d", j=2)
+
+        def scaled_e(pair, on_scalar):
+            tiles["scaled", pair] = work.tile([P, 2, P], F32, name="scaled", tag="scaled", bufs=4)
+            dst, src = tiles["scaled", pair][:], sums_of(pair, 0)
             if on_scalar:
-                nc.scalar.activation(out=es[:, 0:n, :], in_=src, func=ACT.Copy, scale=1.0 / 0.98)
+                nc.scalar.activation(out=dst, in_=src, func=ACT.Copy, scale=1.0 / SHRINK)
             else:
-                nc.vector.tensor_scalar(out=es[:, 0:n, :], in0=src, scalar1=1.0 / 0.98, scalar2=None, op0=ALU.mult)
+                nc.vector.tensor_scalar(out=dst, in0=src, scalar1=1.0 / SHRINK, scalar2=None, op0=ALU.mult)
 
-        def ab_cols(i, j0, j1):
-            return ab[:, i, j0 * P : j1 * P].rearrange("p (j d) -> p j d", d=P)
+        def numerator_and_denominator(pair):
+            e, v = tiles["scaled", pair][:], sums_of(pair, 1)
+            nc.vector.tensor_tensor(out=ratio_part(0, pair), in0=v, in1=e, op=ALU.add)
+            nc.vector.tensor_tensor(out=ratio_part(1, pair), in0=e, in1=v, op=ALU.subtract)
 
-        def v_a(j0, j1):
-            n = j1 - j0
-            nc.vector.tensor_tensor(
-                out=ab_cols(0, j0, j1),
-                in0=st["ev", j0 // 2][:, j0 % 2 : j0 % 2 + n, 1, :],
-                in1=st["es", j0][:, 0:n, :],
-                op=ALU.add,
+        def take_logs(j0, j1):
+            cols = slice(j0 * P, j1 * P)
+            nc.scalar.activation(out=logs[:, :, cols], in_=ratio[:, :, cols], func=ACT.Ln)
+
+        def store(j0, j1):
+            cols = slice(j0 * P, j1 * P)
+            nc.vector.tensor_tensor(out=result[:, cols], in0=logs[:, 0, cols], in1=logs[:, 1, cols], op=ALU.subtract)
+            nc.sync.dma_start(
+                out=out.rearrange("(j p) d -> p j d", p=P)[:, j0:j1, :],
+                in_=result[:, cols].rearrange("p (j d) -> p j d", d=DB),
             )
 
-        def v_b(j0, j1):
-            n = j1 - j0
-            nc.vector.tensor_tensor(
-                out=ab_cols(1, j0, j1),
-                in0=st["es", j0][:, 0:n, :],
-                in1=st["ev", j0 // 2][:, j0 % 2 : j0 % 2 + n, 1, :],
-                op=ALU.subtract,
-            )
-
-        out_rows = out.rearrange("(j p) d -> p j d", p=P)
-
-        def logs(j0, j1):
-            cols = slice(j0 * P, j1 * P)
-            nc.scalar.activation(out=ln_ab[:, :, cols], in_=ab[:, :, cols], func=ACT.Ln)
-
-        def write_out(j0, j1):
-            cols = slice(j0 * P, j1 * P)
-            nc.vector.tensor_tensor(out=out_sb[:, cols], in0=ln_ab[:, 0, cols], in1=ln_ab[:, 1, cols], op=ALU.subtract)
-            nc.sync.dma_start(out=out_rows[:, j0:j1, :], in_=out_sb[:, cols].rearrange("p (j d) -> p j d", d=DB))
-
-        def grouped_in(name, h):
-            if (name, h) not in x_in:
-                new_in((name, h))
-
-        banks_of = {}
-
-        def turn_xa(h, pair):
-            banks_of["xa", h, pair] = turn(xa_bf[h], pair)
-
-        def turn_c(h, pair):
-            banks_of["c", h, pair] = turn(c_sb[h], pair)
-
-        def out_xa(h, pair, on_scalar):
-            grouped_in("xa", h)
-            empty_xa(h, pair, banks_of.pop(("xa", h, pair)), on_scalar)
-
-        def out_c(h, pair):
-            grouped_in("c", h)
-            empty_c(h, pair, banks_of.pop(("c", h, pair)))
-
-        def turn_xb():
-            wx = bank(BF16, 1024)
-            banks_of["xb"] = wx
-            for j in range(TILES):
-                nc.tensor.transpose(wx[:, j * P : (j + 1) * P], xb_sb[:, j, :], ident_bf[:])
-
-        def out_xb():
-            nc.scalar.copy(out=xb_t[:], in_=banks_of.pop("xb")[:])
-
-        def quant_xa(h):
-            quantize(x_in.pop(("xa", h)), x_codes[0][h], x_sc[0][h])
-
-        def quant_c(h):
-            quantize(x_in.pop(("c", h)), x_codes[1][h], x_sc[1][h])
-
-        cast_xa(0, "v", 0, 2)
-        cast_xa(0, "s", 2, 4)
+        scale_xa(0, False, 0, 2)
+        scale_xa(0, True, 2, 4)
         for pair in range(2):
-            turn_xa(0, pair)
+            turn("xa", xa_bf, 0, pair)
         for pair in range(2):
-            turn_c(0, pair)
-        permute(0, 0)
-        out_xa(0, 0, False)
-        out_xa(0, 1, True)
-        permute_scales(0)
-        quant_xa(0)
-        out_c(0, 1)
-        permute(1, 0)
-        out_c(0, 0)
-        permute(1, 1)
-        quant_c(0)
-        for t in range(4):
+            turn("c", c_bf, 0, pair)
+        reorder(w_codes[0], w_raw[0], 0)
+        interleave("xa", 0, 0, False)
+        interleave("xa", 0, 1, True)
+        reorder(w_scales, w_scales_raw, 0)
+        quantize_x(0, 0)
+        interleave("c", 0, 1, True)
+        reorder(w_codes[1], w_raw[1], 0)
+        interleave("c", 0, 0, False)
+        reorder(w_codes[1], w_raw[1], 1)
+        quantize_x(1, 0)
+        for t in range(PACK):
             stage1_pass(0, 0, t, 0)
-        cast_xa(1, "v", 0, 2)
-        cast_xa(1, "s", 2, 4)
-        for t in range(4):
+        scale_xa(1, False, 0, 2)
+        scale_xa(1, True, 2, 4)
+        for t in range(PACK):
             stage1_pass(0, 0, t, 1)
             add_bias(0, 0, t)
-        permute_scales(1)
-        permute(0, 1)
-        slices(0, 1, 0, 0)
+        reorder(w_scales, w_scales_raw, 1)
+        reorder(w_codes[0], w_raw[0], 1)
+
         for pair in range(2):
-            turn_xa(1, pair)
-        out_xa(1, 0, False)
-        out_xa(1, 1, True)
+            turn("xa", xa_bf, 1, pair)
+            interleave("xa", 1, pair, pair == 1)
         leaky(0, 0)
-        slices(0, 1, 0, 2)
-        quant_xa(1)
+        stage1_slices(0, 1, 0, 2)
+        quantize_x(0, 1)
         for pair in range(2):
-            turn_c(1, pair)
-            out_c(1, pair)
-        quant_c(1)
+            turn("c", c_bf, 1, pair)
+            interleave("c", 1, pair, True)
+        quantize_x(1, 1)
         quantize_h(0, 0)
-        slices(0, 1, 2, 4)
+        stage1_slices(0, 1, 2, 4)
         leaky(0, 1)
-        turn_xb()
-        out_xb()
-        slices(1, 0, 0, 4)
+        xb_bank = bank(BF16, TOKENS)
+        for j in range(TILES):
+            nc.tensor.transpose(xb_bank[:, j * P : (j + 1) * P], xb_rows[:, j * DB : (j + 1) * DB], ident_bf[:])
+        nc.scalar.copy(out=xb_turned[:], in_=xb_bank[:])
+
+        stage1_slices(1, 0, 0, PACK)
         quantize_h(0, 1)
         leaky(1, 0)
-        slices(1, 1, 0, 4)
+        stage1_slices(1, 1, 0, PACK)
         leaky(1, 1)
         quantize_h(1, 0)
         quantize_h(1, 1)
+
         for j in range(TILES + 2):
             if j < TILES:
                 stage2("l", j)
-                a_tanh(j)
-                a_exp(j)
+                tanh_l(j)
+                exp_scale(j)
             if 1 <= j <= TILES:
                 stage2("mu", j - 1)
-                v_diff(j - 1)
+                difference(j - 1)
             if j >= 2:
-                product("z", "d", "s", j - 2, Z_ON_GPSIMD)
+                product_z(j - 2)
+
         for j in range(TILES):
             stage2("pl", j)
-            v_max(j)
+            maximum(j)
             if j >= 1:
-                v_sub(j - 1)
-            a_T(j)
+                subtract_maximum(j - 1)
+            tanh_z(j)
             if j >= 2:
-                a_e(j - 2)
+                exp_e(j - 2)
             if j >= 4:
-                sums("e", j - 4)
+                sum_components("e", j - 4)
             if 3 <= j < 7:
-                product("v", "e", "T", j - 3, V_ON_GPSIMD)
-        v_sub(TILES - 1)
-        a_e(TILES - 2)
+                product_v(j - 3)
+
+        subtract_maximum(TILES - 1)
+        exp_e(TILES - 2)
         for j in (4, 5):
-            sums("e", j)
-        a_e(TILES - 1)
-        copy_e(0, 2, True)
+            sum_components("e", j)
+        exp_e(TILES - 1)
+        scaled_e(0, True)
         for j in (0, 1):
-            sums("v", j)
-        mul_tile("v", "e", "T", 4)
-        mul_tile("v", "e", "T", 5)
-        v_a(0, 2)
-        v_b(0, 2)
-        copy_e(2, 4, True)
-        nc.scalar.activation(out=warm[:], in_=warm[:], func=ACT.Ln)
+            sum_components("v", j)
+        product_v(4)
+        product_v(5)
+        numerator_and_denominator(0)
+        scaled_e(1, True)
+        nc.scalar.activation(out=table_probe[:], in_=table_probe[:], func=ACT.Ln)
         for j in (6, 7):
-            sums("e", j)
+            sum_components("e", j)
         for j in (2, 3):
-            sums("v", j)
-        mul_tile("v", "e", "T", 6)
-        copy_e(4, 6, False)
-        mul_tile("v", "e", "T", 7)
-        v_a(2, 4)
-        v_b(2, 4)
-        logs(0, 4)
+            sum_components("v", j)
+        product_v(6)
+        scaled_e(2, False)
+        product_v(7)
+        numerator_and_denominator(1)
+        take_logs(0, 4)
         for j in (4, 5):
-            sums("v", j)
-        copy_e(6, 8, False)
-        v_a(4, 6)
-        v_b(4, 6)
-        logs(4, 6)
+            sum_components("v", j)
+        scaled_e(3, False)
+        numerator_and_denominator(2)
+        take_logs(4, 6)
         for j in (6, 7):
-            sums("v", j)
-        v_a(6, 8)
-        v_b(6, 8)
-        logs(6, 8)
-        write_out(0, 6)
-        write_out(6, 8)
+            sum_components("v", j)
+        numerator_and_denominator(3)
+        take_logs(6, 8)
+        store(0, 6)
+        store(6, 8)

from contextlib import ExitStack

import concourse.mybir as mybir
from concourse.masks import make_identity

F32 = mybir.dt.float32
BF16 = mybir.dt.bfloat16
I32 = mybir.dt.int32
U8 = mybir.dt.uint8
FP8 = mybir.dt.float8_e4m3fn
FP8X4 = mybir.dt.float8_e4m3fn_x4
ACT = mybir.ActivationFunctionType
ALU = mybir.AluOpType
AX = mybir.AxisListType

P = 128
PACK = 4
GROUP = P * PACK
TOKENS, D_IN, F, DB, K = 1024, 512, 1024, 128, 4
J = 3 * K * DB
GROUPS = F // GROUP
TILES = TOKENS // P
HALF_TILES = 4
HALF = HALF_TILES * P
PART = {"pl": 0, "mu": 1, "l": 2}
SHRINK = 0.98

Z_PAIRS_ON_GPSIMD = (2, 3)
V_PAIRS_ON_GPSIMD = (0, 1)

FLOPS = 2 * TOKENS * (2 * D_IN * F + F * J)


def tile_conditionalmixturelogisticcdfcouplingmap_d2p_kernel(
    tc, xa_bytes, xa_scale, xb, c, wa_words, wa_scales, wc_words, wc_scales, b, wo_words, wo_scales, out
):
    nc = tc.nc
    with ExitStack() as ctx:
        keep = ctx.enter_context(tc.tile_pool(name="keep", bufs=1))
        work = ctx.enter_context(tc.tile_pool(name="work", bufs=1))
        psum = ctx.enter_context(tc.psum_pool(name="psum", bufs=1))
        ctx.enter_context(tc.manual_schedule())

        def kept(name, cols, dtype):
            tile = keep.tile([P, cols], dtype, name=name, align_bytes=64)
            return tile

        def kept_twice(name, cols, dtype):
            return [kept(name + str(i), cols, dtype) for i in range(2)]

        def bank(dtype=F32, cols=512):
            tile = psum.tile([P, cols], dtype, name="ring", tag="ring", bufs=6)
            return tile

        xa_u8 = kept_twice("xa_u8", HALF_TILES * D_IN, U8)
        xa_bf = kept_twice("xa_bf", HALF_TILES * D_IN, BF16)
        c_bf = kept_twice("c_bf", HALF_TILES * D_IN, BF16)
        xa_scales = kept("xa_scales", TILES * (D_IN // P), F32)
        xb_rows = kept("xb_rows", TILES * DB, BF16)
        xb_turned = kept("xb_turned", TOKENS, BF16)
        w_raw = kept_twice("w_raw", F, I32)
        w_codes = kept_twice("w_codes", F, I32)
        w_scales_raw = kept("w_scales_raw", F, U8)
        w_scales = kept("w_scales", F, U8)
        wo_codes = kept_twice("wo_codes", J, I32)
        wo_scale_rows = kept("wo_scale_rows", J, U8)
        x_codes = [kept_twice(name + "_codes", HALF, I32) for name in ("xa", "c")]
        x_scale_rows = [kept_twice(name + "_scale_rows", HALF, U8) for name in ("xa", "c")]
        h_codes = [kept_twice("h_codes_g" + str(g), HALF, I32) for g in range(GROUPS)]
        h_scale_rows = [kept_twice("h_scale_rows_g" + str(g), HALF, U8) for g in range(GROUPS)]
        bias_bf = kept("bias_bf", GROUPS * PACK, BF16)
        bias = kept("bias", GROUPS * PACK, F32)
        ident = kept("ident", P, F32)
        ident_bf = kept("ident_bf", P, BF16)
        ratio = keep.tile([P, 2, TOKENS], F32, name="ratio")
        logs = keep.tile([P, 2, TOKENS], F32, name="logs")
        result = kept("result", TOKENS, F32)
        table_probe = kept("table_probe", 1, F32)

        def load_rows(tile, rows, h):
            source = rows.rearrange("(j p) k -> p j k", p=P)[:, h * HALF_TILES : (h + 1) * HALF_TILES, :]
            nc.sync.dma_start(out=tile[:].rearrange("p (j k) -> p j k", k=D_IN), in_=source)

        def load_words(tile, words):
            nc.sync.dma_start(out=tile[:], in_=words.rearrange("p n t -> p (n t)").bitcast(I32))

        def load_scale_rows(queue, tile, scales, first, q):
            rows = slice(32 * q + first, 32 * q + first + 4)
            queue.dma_start(out=tile[rows, :].bitcast(I32), in_=scales[4 * q : 4 * q + 4, :].bitcast(I32))

        nc.vector.memset(w_scales_raw[:].bitcast(I32), 0)
        nc.vector.memset(wo_scale_rows[:].bitcast(I32), 0)
        nc.vector.memset(table_probe[:], 1.0)
        make_identity(nc, ident[:])

        nc.scalar.dma_start(out=xa_scales[:], in_=xa_scale.rearrange("i j -> (i j)").partition_broadcast(P))
        nc.scalar.dma_start(
            out=bias_bf[:].rearrange("p (g t) -> p g t", t=PACK), in_=b.rearrange("(g p t) -> p g t", p=P, t=PACK)
        )
        for q in range(3):
            load_scale_rows(nc.scalar, w_scales_raw, wa_scales[0], 0, q)
        load_rows(xa_u8[0], xa_bytes, 0)
        load_rows(c_bf[0], c, 0)
        load_words(w_raw[0], wa_words[0])
        nc.scalar.activation(out=table_probe[:], in_=table_probe[:], func=ACT.Exp)
        load_scale_rows(nc.sync, w_scales_raw, wa_scales[0], 0, 3)
        for q in range(4):
            load_scale_rows(nc.sync, w_scales_raw, wc_scales[0], 4, q)
        load_words(w_raw[1], wc_words[0])
        load_rows(xa_u8[1], xa_bytes, 1)
        load_rows(c_bf[1], c, 1)
        nc.sync.dma_start(out=xb_rows[:].rearrange("p (j d) -> p j d", d=DB), in_=xb.rearrange("(j p) d -> p j d", p=P))
        for g in range(GROUPS):
            load_words(wo_codes[g], wo_words[g])
        for g in range(GROUPS):
            for q in range(4):
                load_scale_rows(nc.sync, wo_scale_rows, wo_scales[g], 4 * g, q)
        nc.vector.tensor_copy(out=ident_bf[:], in_=ident[:])
        nc.vector.tensor_copy(out=bias[:], in_=bias_bf[:])

        def scale_xa(h, on_scalar, j0, j1):
            for j in range(j0, j1):
                for block in range(D_IN // P):
                    cols = slice(j * D_IN + block * P, j * D_IN + (block + 1) * P)
                    s = (h * HALF_TILES + j) * (D_IN // P) + block
                    values = xa_u8[h][:, cols].bitcast(FP8)
                    factor = xa_scales[:, s : s + 1]
                    if on_scalar:
                        nc.scalar.activation(out=xa_bf[h][:, cols], in_=values, func=ACT.Copy, scale=factor)
                    else:
                        nc.vector.tensor_scalar(
                            out=xa_bf[h][:, cols], in0=values, scalar1=factor, scalar2=None, op0=ALU.mult
                        )

        turned = {}

        def turn(name, source, h, pair):
            w = bank()
            words = source[h][:].bitcast(F32)
            for jj in range(2):
                for u in range(2):
                    first = (2 * pair + jj) * (D_IN // 2)
                    nc.tensor.transpose(
                        w[:, (2 * jj + u) * P : (2 * jj + u + 1) * P], words[:, first + u : first + D_IN // 2 : 2], ident[:]
                    )
            turned[name, h, pair] = w

        grouped = {}

        def grouped_tile(key):
            if key not in grouped:
                grouped[key] = work.tile([P, PACK * HALF], BF16, name="grouped", tag="grouped", bufs=4, align_bytes=64)
            return grouped[key]

        def interleave(name, h, pair, on_scalar):
            tile = grouped_tile((name, h))[:, 2 * pair * D_IN : (2 * pair + 2) * D_IN].bitcast(F32)
            dst = tile.rearrange("p (j n u) -> p j n u", j=2, u=2)
            src = turned.pop((name, h, pair))[:].rearrange("p (j u n) -> p j n u", j=2, u=2)
            if on_scalar:
                nc.scalar.copy(out=dst, in_=src)
            else:
                nc.vector.tensor_copy(out=dst, in_=src)

        def quantize(key, codes, scale_rows):
            source = grouped.pop(key)
            nc.vector.quantize_mx(out=codes[:].bitcast(FP8X4), scales=scale_rows[:], in_=source[:])

        def quantize_x(o, h):
            quantize((("xa", "c")[o], h), x_codes[o][h], x_scale_rows[o][h])

        def quantize_h(h, g):
            quantize(("h", g, h), h_codes[g][h], h_scale_rows[g][h])

        def reorder(dst, src, g):
            cols = slice(GROUP * g, GROUP * (g + 1))
            nc.vector.tensor_copy(
                out=dst[:, cols].rearrange("p (t m) -> p t m", t=PACK), in_=src[:, cols].rearrange("p (m t) -> p t m", t=PACK)
            )

        stage1_banks = {}
        y_tiles = {}

        def stage1_pass(h, g, t, o):
            cols = slice((PACK * g + t) * P, (PACK * g + t + 1) * P)
            if o == 0:
                stage1_banks[h, g, t] = bank()
            nc.tensor.matmul_mx(
                out=stage1_banks[h, g, t][:],
                lhsT=w_codes[o][:, cols].bitcast(FP8X4),
                lhsT_scale=w_scales[4 * o : P, cols],
                rhs=x_codes[o][h][:].bitcast(FP8X4),
                rhs_scale=x_scale_rows[o][h][:],
                start=(o == 0),
                stop=(o == 1),
            )

        def add_bias(h, g, t):
            if (h, g) not in y_tiles:
                y_tiles[h, g] = work.tile([P, PACK, HALF], F32, name="y", tag="y", bufs=3)
            nc.scalar.activation(
                out=y_tiles[h, g][:, t, :],
                in_=stage1_banks.pop((h, g, t))[:],
                func=ACT.Identity,
                bias=bias[:, PACK * g + t : PACK * g + t + 1],
            )

        def stage1_slices(h, g, t0, t1):
            for t in range(t0, t1):
                stage1_pass(h, g, t, 0)
                stage1_pass(h, g, t, 1)
                add_bias(h, g, t)

        def leaky(h, g):
            y = y_tiles.pop((h, g))[:].rearrange("p t n -> p n t")
            dst = grouped_tile(("h", g, h))[:].rearrange("p (n t) -> p n t", t=PACK)
            nc.vector.scalar_tensor_tensor(out=dst, in0=y, scalar=0.2, in1=y, op0=ALU.mult, op1=ALU.max)

        banks = {}

        def stage2(name, j):
            h, jj = divmod(j, HALF_TILES)
            tokens = slice(jj * P, (jj + 1) * P)
            w = bank()
            banks[name, j] = w
            for k in range(K):
                first = (PART[name] * K + k) * DB
                cols = slice(first, first + DB)
                for g in range(GROUPS):
                    nc.tensor.matmul_mx(
                        out=w[:, k * P : (k + 1) * P],
                        lhsT=wo_codes[g][:, cols].bitcast(FP8X4),
                        lhsT_scale=wo_scale_rows[4 * g : P, cols],
                        rhs=h_codes[g][h][:, tokens].bitcast(FP8X4),
                        rhs_scale=h_scale_rows[g][h][:, tokens],
                        start=(g == 0),
                        stop=(g == GROUPS - 1),
                    )

        def by_component(ap):
            return ap.rearrange("p (k n) -> p k n", k=K)

        def over_components(ap):
            return ap.unsqueeze(1).to_broadcast([P, K, P])

        depth = {"t": 3, "q": 4, "s": 3, "diff": 3, "z": 3, "T": 4, "e": 4, "v": 3}
        tiles = {}

        def tile_of(name, j):
            if (name, j) not in tiles:
                tiles[name, j] = work.tile([P, K * P], F32, name=name, tag=name, bufs=depth[name])
            return tiles[name, j][:]

        def pair_of(name, pair):
            if (name, pair) not in tiles:
                tiles[name, pair] = work.tile([P, 2, K * P], F32, name=name, tag=name, bufs=depth[name])
            return tiles[name, pair]

        def half_of(name, j):
            return pair_of(name, j // 2)[:, j % 2, :]

        def tanh_l(j):
            nc.scalar.activation(out=tile_of("t", j), in_=banks.pop(("l", j))[:], func=ACT.Tanh)

        def exp_scale(j):
            nc.scalar.activation(out=half_of("s", j), in_=tile_of("t", j), func=ACT.Exp, scale=-1.0)

        def difference(j):
            nc.vector.tensor_tensor(
                out=by_component(half_of("diff", j)),
                in0=by_component(banks.pop(("mu", j))[:]),
                in1=over_components(xb_turned[:, j * P : (j + 1) * P]),
                op=ALU.subtract,
            )

        def maximum(j):
            tiles["max", j] = work.tile([P, P], F32, name="max", tag="max", bufs=4)
            nc.vector.tensor_reduce(
                out=tiles["max", j][:],
                in_=banks["pl", j][:].rearrange("p (k n) -> p n k", k=K),
                axis=AX.X,
                op=ALU.max,
            )

        def subtract_maximum(j):
            nc.vector.tensor_tensor(
                out=by_component(tile_of("q", j)),
                in0=by_component(banks.pop(("pl", j))[:]),
                in1=over_components(tiles.pop(("max", j))[:]),
                op=ALU.subtract,
            )

        def exp_e(j):
            nc.scalar.activation(out=half_of("e", j), in_=tile_of("q", j), func=ACT.Exp)

        def tanh_z(j):
            nc.scalar.activation(out=half_of("T", j), in_=half_of("z", j), func=ACT.Tanh, scale=-0.5)

        def product(result_name, a, b_name, j, pairs_on_gpsimd):
            if j // 2 not in pairs_on_gpsimd:
                nc.vector.tensor_tensor(
                    out=half_of(result_name, j), in0=half_of(a, j), in1=half_of(b_name, j), op=ALU.mult
                )
            elif j % 2 == 1:
                nc.gpsimd.tensor_tensor(
                    out=pair_of(result_name, j // 2)[:],
                    in0=pair_of(a, j // 2)[:],
                    in1=pair_of(b_name, j // 2)[:],
                    op=ALU.mult,
                )

        def product_z(j):
            product("z", "diff", "s", j, Z_PAIRS_ON_GPSIMD)

        def product_v(j):
            product("v", "e", "T", j, V_PAIRS_ON_GPSIMD)

        sums_banks = {}

        def sum_components(name, j):
            pair = j // 2
            if pair not in sums_banks:
                if j < HALF_TILES:
                    sums_banks[pair] = psum.tile([P, 512], F32, name="sums", tag="sums", bufs=2)
                else:
                    sums_banks[pair] = bank()
            first = (2 * (j % 2) + ("e", "v").index(name)) * P
            for k in range(K):
                nc.tensor.matmul(
                    sums_banks[pair][:, first : first + P],
                    lhsT=half_of(name, j)[:, k * P : (k + 1) * P],
                    rhs=ident[:],
                    is_transpose=True,
                    start=(k == 0),
                    stop=(k == K - 1),
                )

        def sums_of(pair, i):
            return sums_banks[pair][:].rearrange("p (j i d) -> p j i d", j=2, i=2)[:, :, i, :]

        def ratio_part(i, pair):
            return ratio[:, i, 2 * pair * P : (2 * pair + 2) * P].rearrange("p (j d) -> p j d", j=2)

        def scaled_e(pair, on_scalar):
            tiles["scaled", pair] = work.tile([P, 2, P], F32, name="scaled", tag="scaled", bufs=4)
            dst, src = tiles["scaled", pair][:], sums_of(pair, 0)
            if on_scalar:
                nc.scalar.activation(out=dst, in_=src, func=ACT.Copy, scale=1.0 / SHRINK)
            else:
                nc.vector.tensor_scalar(out=dst, in0=src, scalar1=1.0 / SHRINK, scalar2=None, op0=ALU.mult)

        def numerator_and_denominator(pair):
            e, v = tiles["scaled", pair][:], sums_of(pair, 1)
            nc.vector.tensor_tensor(out=ratio_part(0, pair), in0=v, in1=e, op=ALU.add)
            nc.vector.tensor_tensor(out=ratio_part(1, pair), in0=e, in1=v, op=ALU.subtract)

        def take_logs(j0, j1):
            cols = slice(j0 * P, j1 * P)
            nc.scalar.activation(out=logs[:, :, cols], in_=ratio[:, :, cols], func=ACT.Ln)

        def store(j0, j1):
            cols = slice(j0 * P, j1 * P)
            nc.vector.tensor_tensor(out=result[:, cols], in0=logs[:, 0, cols], in1=logs[:, 1, cols], op=ALU.subtract)
            nc.sync.dma_start(
                out=out.rearrange("(j p) d -> p j d", p=P)[:, j0:j1, :],
                in_=result[:, cols].rearrange("p (j d) -> p j d", d=DB),
            )

        scale_xa(0, False, 0, 2)
        scale_xa(0, True, 2, 4)
        for pair in range(2):
            turn("xa", xa_bf, 0, pair)
        for pair in range(2):
            turn("c", c_bf, 0, pair)
        reorder(w_codes[0], w_raw[0], 0)
        interleave("xa", 0, 0, False)
        interleave("xa", 0, 1, True)
        reorder(w_scales, w_scales_raw, 0)
        quantize_x(0, 0)
        interleave("c", 0, 1, True)
        reorder(w_codes[1], w_raw[1], 0)
        interleave("c", 0, 0, False)
        reorder(w_codes[1], w_raw[1], 1)
        quantize_x(1, 0)
        for t in range(PACK):
            stage1_pass(0, 0, t, 0)
        scale_xa(1, False, 0, 2)
        scale_xa(1, True, 2, 4)
        for t in range(PACK):
            stage1_pass(0, 0, t, 1)
            add_bias(0, 0, t)
        reorder(w_scales, w_scales_raw, 1)
        reorder(w_codes[0], w_raw[0], 1)

        for pair in range(2):
            turn("xa", xa_bf, 1, pair)
            interleave("xa", 1, pair, pair == 1)
        leaky(0, 0)
        stage1_slices(0, 1, 0, 2)
        quantize_x(0, 1)
        for pair in range(2):
            turn("c", c_bf, 1, pair)
            interleave("c", 1, pair, True)
        quantize_x(1, 1)
        quantize_h(0, 0)
        stage1_slices(0, 1, 2, 4)
        leaky(0, 1)
        xb_bank = bank(BF16, TOKENS)
        for j in range(TILES):
            nc.tensor.transpose(xb_bank[:, j * P : (j + 1) * P], xb_rows[:, j * DB : (j + 1) * DB], ident_bf[:])
        nc.scalar.copy(out=xb_turned[:], in_=xb_bank[:])

        stage1_slices(1, 0, 0, PACK)
        quantize_h(0, 1)
        leaky(1, 0)
        stage1_slices(1, 1, 0, PACK)
        leaky(1, 1)
        quantize_h(1, 0)
        quantize_h(1, 1)

        for j in range(TILES + 2):
            if j < TILES:
                stage2("l", j)
                tanh_l(j)
                exp_scale(j)
            if 1 <= j <= TILES:
                stage2("mu", j - 1)
                difference(j - 1)
            if j >= 2:
                product_z(j - 2)

        for j in range(TILES):
            stage2("pl", j)
            maximum(j)
            if j >= 1:
                subtract_maximum(j - 1)
            tanh_z(j)
            if j >= 2:
                exp_e(j - 2)
            if j >= 4:
                sum_components("e", j - 4)
            if 3 <= j < 7:
                product_v(j - 3)

        subtract_maximum(TILES - 1)
        exp_e(TILES - 2)
        for j in (4, 5):
            sum_components("e", j)
        exp_e(TILES - 1)
        scaled_e(0, True)
        for j in (0, 1):
            sum_components("v", j)
        product_v(4)
        product_v(5)
        numerator_and_denominator(0)
        scaled_e(1, True)
        nc.scalar.activation(out=table_probe[:], in_=table_probe[:], func=ACT.Ln)
        for j in (6, 7):
            sum_components("e", j)
        for j in (2, 3):
            sum_components("v", j)
        product_v(6)
        scaled_e(2, False)
        product_v(7)
        numerator_and_denominator(1)
        take_logs(0, 4)
        for j in (4, 5):
            sum_components("v", j)
        scaled_e(3, False)
        numerator_and_denominator(2)
        take_logs(4, 6)
        for j in (6, 7):
            sum_components("v", j)
        numerator_and_denominator(3)
        take_logs(6, 8)
        store(0, 6)
        store(6, 8)
